import numpy as np
import ml_dtypes


def mxq(x, axis, fmt="e4m3"):
    dtype, down = {"e4m3": (ml_dtypes.float8_e4m3fn, 7), "e5m2": (ml_dtypes.float8_e5m2, 14)}[fmt]
    v = np.moveaxis(np.asarray(x, np.float32).astype(ml_dtypes.bfloat16).astype(np.float64), axis, -1)
    blocks = v.reshape(v.shape[:-1] + (-1, 32))
    amax = np.abs(blocks).max(-1, keepdims=True)
    byte = np.maximum(np.where(amax > 0, np.frexp(amax)[1] - 1 + 127, 0) - down, 1)
    scale = np.exp2(byte - 127.0)
    codes = (blocks / scale).astype(np.float32).astype(dtype).astype(np.float64)
    return np.moveaxis((codes * scale).reshape(v.shape), -1, axis)


WIDE = False


def mx_kscale(k):
    if not WIDE:
        return np.ones(k)
    levels = np.array([18, -18])
    if k % 512:
        return np.exp2(np.random.permutation(np.resize(levels, k // 32))).repeat(32)
    a = np.empty((k // 512, 16))
    for p in range(k // 512):
        a[p, :8] = np.random.permutation(np.resize(levels, 8))
        for g in range(8):
            far = levels[np.abs(levels - a[p, g]) >= 10]
            a[p, g + 8] = far[np.random.randint(len(far))]
    return np.exp2(a.ravel()).repeat(32)


def f64(x):
    return np.asarray(x).astype(np.float64)


def striped(idx):
    return np.tile(np.asarray(idx).reshape(-1, 16).T, (8, 1)).astype(np.uint16)


def unstriped(offs):
    return offs[:16].T.reshape(-1).astype(np.int64)


E2M1 = np.array([0.0, 0.5, 1.0, 1.5, 2.0, 3.0, 4.0, 6.0, -0.0, -0.5, -1.0, -1.5, -2.0, -3.0, -4.0, -6.0])


def pack_weight(w, fmt):
    k, n = w.shape
    w = f64(np.asarray(w, np.float32).astype(ml_dtypes.bfloat16)).reshape(k // 32, 32, n)
    amax = np.abs(w).max(1)
    if fmt == "e4m3":
        byte = np.frexp(amax)[1] - 1 + 127 - 7
    else:
        mant, ex = np.frexp(amax / 6.0)
        byte = np.where(mant > 0.5, ex, ex - 1) + 127
    byte = np.clip(np.where(amax > 0, byte, 1), 1, 254)
    scaled = (w * np.exp2(127.0 - byte)[:, None, :]).reshape(k, n).astype(np.float32)
    by_word = np.ascontiguousarray(scaled.reshape(k // 512, 128, 4, n).transpose(0, 1, 3, 2))
    if fmt == "e4m3":
        words = by_word.astype(ml_dtypes.float8_e4m3fn).view(np.uint8)
    else:
        c = by_word.astype(ml_dtypes.float4_e2m1fn).view(np.uint8) & 0xF
        words = (c[..., 0::2] | (c[..., 1::2] << 4)).reshape(k // 512, 128, 2 * n)
    return np.ascontiguousarray(words), np.ascontiguousarray(byte.astype(np.uint8).reshape(k // 512, 16, n))


def unpack_weight(words, scales, fmt):
    g, _, n = scales.shape
    words = np.ascontiguousarray(words).reshape(g, 128, n, -1)
    if fmt == "e4m3":
        vals = words.view(ml_dtypes.float8_e4m3fn).astype(np.float64)
    else:
        nib = np.empty((g, 128, n, 4), np.uint8)
        nib[..., 0::2] = words & 0xF
        nib[..., 1::2] = words >> 4
        vals = E2M1[nib]
    vals = vals * np.repeat(np.exp2(scales.astype(np.float64) - 127.0), 8, axis=1)[..., None]
    return vals.transpose(0, 1, 3, 2).reshape(g * 512, n)


def planes(y):
    n, m = y.shape
    v = y.astype(np.float32).astype(ml_dtypes.bfloat16).astype(np.float64).reshape(n // 32, 32, m)
    top = np.abs(v).max(1)
    byte = np.clip(np.where(top > 0, np.frexp(top)[1] - 1 + 127 - 7, 1), 1, 254)
    codes = (v * np.exp2(127.0 - byte)[:, None, :]).reshape(n, m).astype(np.float32).astype(ml_dtypes.float8_e4m3fn).view(np.uint8)
    words = codes.reshape(n // 512, 128, 4, m).transpose(0, 1, 3, 2)
    return np.ascontiguousarray(words), np.ascontiguousarray(byte.astype(np.uint8).reshape(n // 512, 16, m))


def setup_inputs():
    n = np.random.standard_normal
    uni = np.random.uniform
    idx = np.random.permutation(1024)[:512]
    f_d = mx_kscale(512)
    f_r = mx_kscale(512)
    Pj_ = pack_weight(n((512, 512)) / np.sqrt(512) / f_d[:, None], "e2m1")
    return {
        "xT": (n((512, 512)) * f_d[:, None] * f_r[None, :]).astype(np.float32),
        "G": (n((512, 512)) / np.sqrt(512) / f_r[:, None]).astype(np.float32),
        "Pj_words": Pj_[0],
        "Pj_scales": Pj_[1],
        "mT": (n((512, 1024))).astype(np.float32),
        "offs": striped(idx),
    }


def reference(xT, G, Pj_words, Pj_scales, mT, offs):
    idx = unstriped(offs)
    Pj = unpack_weight(Pj_words, Pj_scales, "e2m1")
    m = f64(mT)[:, idx]
    dw = mxq(f64(xT), 1, "e4m3") @ mxq(f64(G), 0, "e5m2")
    q = Pj.T @ mxq(dw, 0, "e4m3")
    nm = 0.9 * m + q
    out_0 = f64(mT)
    out_0[:, idx] = nm
    return (out_0,) + planes(out_0)

@@ -1,0 +1,210 @@
+from contextlib import ExitStack
+
+import concourse.mybir as mybir
+from concourse.masks import make_identity
+
+F32 = mybir.dt.float32
+BF16 = mybir.dt.bfloat16
+I32 = mybir.dt.int32
+U32 = mybir.dt.uint32
+U16 = mybir.dt.uint16
+U8 = mybir.dt.uint8
+E4M3 = mybir.dt.float8_e4m3fn_x4
+E5M2 = mybir.dt.float8_e5m2_x4
+E2M1 = mybir.dt.float4_e2m1fn_x4
+MULT = mybir.AluOpType.mult
+ADD = mybir.AluOpType.add
+
+P = 128
+LANES = 4
+D = R = K = SLOTS = 512
+COLS = 1024
+HALF = SLOTS // 2
+DECAY = 0.9
+FLOPS = 2 * D * R * SLOTS + 2 * K * D * SLOTS
+
+
+def tile_attend_glowmom_pl_kernel(
+    tc, xT, G, Pj_words, Pj_scales, mT, offs, out_0, out_1, out_2
+):
+    nc = tc.nc
+    with ExitStack() as ctx:
+        keep = ctx.enter_context(tc.tile_pool(name="keep", bufs=1))
+        psum = ctx.enter_context(tc.psum_pool(name="psum", bufs=1))
+
+        def sb(name, shape, dtype, after=None):
+            return keep.tile(shape, dtype, name=name, tag=after or name, align_bytes=64)
+
+        offsets = keep.tile([P, SLOTS // 16], U16, name="offsets")
+        ident = sb("ident", [P, P], F32)
+        x_raw = [sb("x_raw%d" % h, [P, 2, R], F32) for h in range(2)]
+        g_raw = [sb("g_raw%d" % h, [P, LANES, HALF], F32) for h in range(2)]
+        pj_raw = sb("pj_raw", [P, 2 * K], U8)
+        pjs_raw = sb("pjs_raw", [P, K], U8)
+        m_src = [sb("m_src%d" % j, [P, COLS], F32) for j in range(LANES)]
+        m_new = [sb("m_new%d" % j, [P, COLS], F32) for j in range(LANES)]
+
+        m_rows = mT.rearrange("(p j) t -> p j t", j=LANES)
+        out_rows = out_0.rearrange("(p j) t -> p j t", j=LANES)
+        g_rows = G.rearrange("(p j) i -> p j i", j=LANES)
+        x_rows = xT.rearrange("(c p) r -> p c r", p=P)
+
+        nc.gpsimd.memset(pjs_raw[:].bitcast(I32), 0)
+        make_identity(nc, ident[:])
+
+        nc.sync.dma_start(out=x_raw[0][:], in_=x_rows[:, 0:2, :])
+        nc.sync.dma_start(out=pj_raw[:].bitcast(I32), in_=Pj_words[0].bitcast(I32))
+        for q in range(4):
+            nc.sync.dma_start(
+                out=pjs_raw[32 * q : 32 * q + 4, :].bitcast(I32),
+                in_=Pj_scales[0, 4 * q : 4 * q + 4, :].bitcast(I32),
+            )
+        nc.sync.dma_start(out=x_raw[1][:], in_=x_rows[:, 2:4, :])
+        for h in range(2):
+            nc.sync.dma_start(out=g_raw[h][:], in_=g_rows[:, :, h * HALF : (h + 1) * HALF])
+        nc.sync.dma_start(offsets[:], offs)
+        for j in range(LANES):
+            nc.sync.dma_start(out=m_src[j][:], in_=m_rows[:, j, :])
+        for j in range(LANES):
+            nc.sync.dma_start(out=m_new[j][:], in_=m_rows[:, j, :])
+
+        def turn_and_quantize(name, sorted_tiles, codes, scales):
+            bank = psum.tile([P, 2, 2, P], F32, name=name + "_bank", tag="turn", bufs=2)
+            for c in range(2):
+                words = sorted_tiles[c][:].bitcast(F32)
+                for u in range(2):
+                    nc.tensor.transpose(bank[:, c, u, :], words[:, u * P : (u + 1) * P], ident[:])
+            grouped = sb(name + "_grouped", [P, 2 * P * 2], F32)
+            nc.scalar.copy(
+                out=grouped[:].rearrange("p (c n u) -> p c n u", c=2, u=2),
+                in_=bank[:].rearrange("p c u n -> p c n u"),
+            )
+            nc.vector.quantize_mx(out=codes.bitcast(E4M3), scales=scales, in_=grouped[:].bitcast(BF16))
+
+        def sort_pairs(copy, dst, src):
+            copy(
+                out=dst.rearrange("a (u p e) -> a u p e", u=2, e=2),
+                in_=src.rearrange("a (p u e) -> a u p e", u=2, e=2),
+            )
+
+        x_codes = sb("x_codes", [P, D], U32)
+        x_scales = sb("x_scales", [P, D], U8)
+
+        def quantize_x(h):
+            tiles = []
+            for c in range(2):
+                t = sb("x_sorted%d%d" % (h, c), [P, R], BF16)
+                sort_pairs(nc.vector.tensor_copy, t[:], x_raw[h][:, c, :])
+                tiles.append(t)
+            cols = slice(h * 2 * P, (h + 1) * 2 * P)
+            turn_and_quantize("x%d" % h, tiles, x_codes[:, cols], x_scales[:, cols])
+
+        quantize_x(0)
+        pj_words = sb("pj_words", [P, 2 * K], U8)
+        pj_scales = sb("pj_scales", [P, K], U8)
+        nc.vector.tensor_copy(
+            out=pj_words[:].bitcast(U16).rearrange("p (j m) -> p j m", j=LANES),
+            in_=pj_raw[:].bitcast(U16).rearrange("p (m j) -> p j m", j=LANES),
+        )
+        nc.vector.tensor_copy(
+            out=pj_scales[:].rearrange("p (j m) -> p j m", j=LANES),
+            in_=pjs_raw[:].rearrange("p (m j) -> p j m", j=LANES),
+        )
+
+        quantize_x(1)
+
+        g_codes = [sb("g_codes%d" % h, [P, HALF], U32) for h in range(2)]
+        g_scales = [sb("g_scales%d" % h, [P, HALF], U8) for h in range(2)]
+        for h in range(2):
+            grouped = sb("g_grouped%d" % h, [P, HALF * LANES], BF16, after=(None, "x1_grouped")[h])
+            nc.vector.tensor_copy(
+                out=grouped[:].rearrange("p (c i t) -> p c t i", i=4, t=LANES),
+                in_=g_raw[h][:].rearrange("p t (c i) -> p c t i", i=4),
+            )
+            nc.vector.quantize_mx(out=g_codes[h][:].bitcast(E5M2), scales=g_scales[h][:], in_=grouped[:])
+
+        dw_sorted = []
+        for n in range(4):
+            h, cols = n // 2, slice(n % 2 * P, (n % 2 + 1) * P)
+            bank = psum.tile([P, D], F32, name="dw_bank%d" % n, tag="dw", bufs=2)
+            nc.tensor.matmul_mx(
+                out=bank[:],
+                lhsT=g_codes[h][:, cols].bitcast(E5M2),
+                lhsT_scale=g_scales[h][:, cols],
+                rhs=x_codes[:].bitcast(E4M3),
+                rhs_scale=x_scales[:],
+                start=True,
+                stop=True,
+            )
+            t = sb("dw_sorted%d" % n, [P, D], BF16)
+            sort_pairs(nc.scalar.copy, t[:], bank[:])
+            dw_sorted.append(t)
+
+        q_banks = [psum.tile([P, SLOTS], F32, name="q_bank%d" % j) for j in range(LANES)]
+        for h in range(2):
+            codes = sb("dw_codes%d" % h, [P, HALF], U32)
+            scales = sb("dw_scales%d" % h, [P, HALF], U8)
+            turn_and_quantize("dw%d" % h, dw_sorted[2 * h : 2 * h + 2], codes[:], scales[:])
+            for j in range(LANES):
+                nc.tensor.matmul_mx(
+                    out=q_banks[j][:, h * HALF : (h + 1) * HALF],
+                    lhsT=pj_words[:, 2 * P * j : 2 * P * (j + 1)].bitcast(E2M1),
+                    lhsT_scale=pj_scales[:, P * j : P * (j + 1)],
+                    rhs=codes[:].bitcast(E4M3),
+                    rhs_scale=scales[:],
+                    start=True,
+                    stop=True,
+                )
+
+        picked = []
+        for j, after in enumerate(["x1_grouped", "m_src0", "dw1_grouped", "m_src2"]):
+            t = sb("picked%d" % j, [P, SLOTS], F32, after=after)
+            nc.vector.tensor_copy(t[:], m_src[j][:].indirect(offsets[:]))
+            picked.append(t)
+
+        q_sb = [sb("q_sb%d" % j, [P, SLOTS], F32) for j in range(LANES)]
+        decayed = []
+        for j, after in enumerate(["dw_sorted3", "dw_codes1", "m_src0", "dw1_grouped"]):
+            nc.scalar.copy(out=q_sb[j][:], in_=q_banks[j][:])
+            t = sb("decayed%d" % j, [P, SLOTS], F32, after=after)
+            nc.scalar.mul(t[:], picked[j][:], DECAY)
+            decayed.append(t)
+
+        def scatter(j):
+            nc.vector.tensor_tensor(m_new[j][:].indirect(offsets[:]), decayed[j][:], q_sb[j][:], ADD)
+
+        WIDE = COLS // 2
+        y_grouped = [sb("y_grouped%d" % s, [P, WIDE, LANES], BF16) for s in range(2)]
+        y_codes = [sb("y_codes%d" % s, [P, WIDE], U32) for s in range(2)]
+        y_scales = sb("y_scales", [P, COLS], U8)
+
+        def hand_out(j):
+            nc.sync.dma_start(out=out_rows[:, j, :], in_=m_new[j][:])
+            left, right = m_new[j][:, :WIDE], m_new[j][:, WIDE:]
+            if j == 2:
+                nc.scalar.copy(out=y_grouped[0][:, :, 2:4], in_=left.unsqueeze(2).to_broadcast([P, WIDE, 2]))
+            elif j == 3:
+                nc.vector.tensor_copy(out=y_grouped[0][:, :, j], in_=left)
+            else:
+                nc.scalar.copy(out=y_grouped[0][:, :, j], in_=left)
+            nc.scalar.copy(out=y_grouped[1][:, :, j], in_=right)
+
+        for j in range(LANES):
+            scatter(j)
+            hand_out(j)
+
+        words_out = out_1[0].rearrange("p n t -> p (n t)").bitcast(I32)
+        for s in range(2):
+            cols = slice(s * WIDE, (s + 1) * WIDE)
+            nc.vector.quantize_mx(
+                out=y_codes[s][:].bitcast(E4M3),
+                scales=y_scales[:, cols],
+                in_=y_grouped[s][:].rearrange("p n t -> p (n t)"),
+            )
+            nc.sync.dma_start(out=words_out[:, cols], in_=y_codes[s][:].bitcast(I32))
+        for q in range(4):
+            queue = nc.sync if q % 2 == 0 else nc.scalar
+            queue.dma_start(
+                out=out_2[0, 4 * q : 4 * q + 4, :].bitcast(I32),
+                in_=y_scales[32 * q : 32 * q + 4, :].bitcast(I32),
+            )

@@ -37,7 +37,9 @@ def tile_attend_glowmom_pl_kernel(
 
         offsets = keep.tile([P, SLOTS // 16], U16, name="offsets")
         ident = sb("ident", [P, P], F32)
-        x_raw = [sb("x_raw%d" % h, [P, 2, R], F32) for h in range(2)]
+        x_head = sb("x_head", [P, 2, R], F32)
+        x_tail = [sb("x_tail%d" % c, [P, R], F32) for c in range(2)]
+        x_raw = [x_head[:, 0, :], x_head[:, 1, :], x_tail[0][:], x_tail[1][:]]
         g_raw = [sb("g_raw%d" % h, [P, LANES, HALF], F32) for h in range(2)]
         pj_raw = sb("pj_raw", [P, 2 * K], U8)
         pjs_raw = sb("pjs_raw", [P, K], U8)
@@ -47,19 +49,20 @@ def tile_attend_glowmom_pl_kernel(
         m_rows = mT.rearrange("(p j) t -> p j t", j=LANES)
         out_rows = out_0.rearrange("(p j) t -> p j t", j=LANES)
         g_rows = G.rearrange("(p j) i -> p j i", j=LANES)
-        x_rows = xT.rearrange("(c p) r -> p c r", p=P)
+        x_rows = xT.rearrange("(p c) r -> p c r", c=LANES)
 
         nc.gpsimd.memset(pjs_raw[:].bitcast(I32), 0)
         make_identity(nc, ident[:])
 
-        nc.sync.dma_start(out=x_raw[0][:], in_=x_rows[:, 0:2, :])
+        nc.sync.dma_start(out=x_head[:], in_=x_rows[:, 0:2, :])
+        for c in range(2):
+            nc.sync.dma_start(out=x_tail[c][:], in_=x_rows[:, 2 + c, :])
         nc.sync.dma_start(out=pj_raw[:].bitcast(I32), in_=Pj_words[0].bitcast(I32))
         for q in range(4):
-            nc.sync.dma_start(
+            nc.scalar.dma_start(
                 out=pjs_raw[32 * q : 32 * q + 4, :].bitcast(I32),
                 in_=Pj_scales[0, 4 * q : 4 * q + 4, :].bitcast(I32),
             )
-        nc.sync.dma_start(out=x_raw[1][:], in_=x_rows[:, 2:4, :])
         for h in range(2):
             nc.sync.dma_start(out=g_raw[h][:], in_=g_rows[:, :, h * HALF : (h + 1) * HALF])
         nc.sync.dma_start(offsets[:], offs)
@@ -68,17 +71,19 @@ def tile_attend_glowmom_pl_kernel(
         for j in range(LANES):
             nc.sync.dma_start(out=m_new[j][:], in_=m_rows[:, j, :])
 
-        def turn_and_quantize(name, sorted_tiles, codes, scales):
-            bank = psum.tile([P, 2, 2, P], F32, name=name + "_bank", tag="turn", bufs=2)
-            for c in range(2):
+        def turn(name, sorted_tiles, words_out):
+            n = len(sorted_tiles)
+            bank = psum.tile([P, n, 2, P], F32, name=name + "_bank", tag="turn", bufs=3)
+            for c in range(n):
                 words = sorted_tiles[c][:].bitcast(F32)
                 for u in range(2):
                     nc.tensor.transpose(bank[:, c, u, :], words[:, u * P : (u + 1) * P], ident[:])
-            grouped = sb(name + "_grouped", [P, 2 * P * 2], F32)
             nc.scalar.copy(
-                out=grouped[:].rearrange("p (c n u) -> p c n u", c=2, u=2),
+                out=words_out.rearrange("p (c n u) -> p c n u", c=n, u=2),
                 in_=bank[:].rearrange("p c u n -> p c n u"),
             )
+
+        def quantize(codes, scales, grouped):
             nc.vector.quantize_mx(out=codes.bitcast(E4M3), scales=scales, in_=grouped[:].bitcast(BF16))
 
         def sort_pairs(copy, dst, src):
@@ -91,15 +96,16 @@ def tile_attend_glowmom_pl_kernel(
         x_scales = sb("x_scales", [P, D], U8)
 
         def quantize_x(h):
-            tiles = []
+            grouped = sb("x%d_grouped" % h, [P, 4 * P], F32)
             for c in range(2):
                 t = sb("x_sorted%d%d" % (h, c), [P, R], BF16)
-                sort_pairs(nc.vector.tensor_copy, t[:], x_raw[h][:, c, :])
-                tiles.append(t)
+                sort_pairs(nc.vector.tensor_copy if h + c else nc.scalar.copy, t[:], x_raw[2 * h + c])
+                turn("x%d%d" % (h, c), [t], grouped[:, 2 * P * c : 2 * P * (c + 1)])
             cols = slice(h * 2 * P, (h + 1) * 2 * P)
-            turn_and_quantize("x%d" % h, tiles, x_codes[:, cols], x_scales[:, cols])
+            quantize(x_codes[:, cols], x_scales[:, cols], grouped)
 
         quantize_x(0)
+        quantize_x(1)
         pj_words = sb("pj_words", [P, 2 * K], U8)
         pj_scales = sb("pj_scales", [P, K], U8)
         nc.vector.tensor_copy(
@@ -111,22 +117,29 @@ def tile_attend_glowmom_pl_kernel(
             in_=pjs_raw[:].rearrange("p (m j) -> p j m", j=LANES),
         )
 
-        quantize_x(1)
-
         g_codes = [sb("g_codes%d" % h, [P, HALF], U32) for h in range(2)]
         g_scales = [sb("g_scales%d" % h, [P, HALF], U8) for h in range(2)]
         for h in range(2):
-            grouped = sb("g_grouped%d" % h, [P, HALF * LANES], BF16, after=(None, "x1_grouped")[h])
-            nc.vector.tensor_copy(
-                out=grouped[:].rearrange("p (c i t) -> p c t i", i=4, t=LANES),
-                in_=g_raw[h][:].rearrange("p t (c i) -> p c t i", i=4),
-            )
-            nc.vector.quantize_mx(out=g_codes[h][:].bitcast(E5M2), scales=g_scales[h][:], in_=grouped[:])
+            grouped = sb("g_grouped%d" % h, [P, HALF * LANES], BF16, after="x%d_grouped" % h)
+            dst = grouped[:].rearrange("p (c i t) -> p c t i", i=4, t=LANES)
+            src = g_raw[h][:].rearrange("p t (c i) -> p c t i", i=4)
+            if h == 0:
+                nc.vector.tensor_copy(out=dst[:, :32], in_=src[:, :32])
+                nc.scalar.copy(out=dst[:, 32:], in_=src[:, 32:])
+            else:
+                nc.vector.tensor_copy(out=dst, in_=src)
+            for first, last in ([(0, P), (P, HALF)] if h == 0 else [(0, HALF)]):
+                nc.vector.quantize_mx(
+                    out=g_codes[h][:, first:last].bitcast(E5M2),
+                    scales=g_scales[h][:, first:last],
+                    in_=grouped[:, LANES * first : LANES * last],
+                )
 
         dw_sorted = []
-        for n in range(4):
+
+        def first_product(n):
             h, cols = n // 2, slice(n % 2 * P, (n % 2 + 1) * P)
-            bank = psum.tile([P, D], F32, name="dw_bank%d" % n, tag="dw", bufs=2)
+            bank = psum.tile([P, D], F32, name="dw_bank%d" % n, tag="bank%d" % n)
             nc.tensor.matmul_mx(
                 out=bank[:],
                 lhsT=g_codes[h][:, cols].bitcast(E5M2),
@@ -137,74 +150,107 @@ def tile_attend_glowmom_pl_kernel(
                 stop=True,
             )
             t = sb("dw_sorted%d" % n, [P, D], BF16)
-            sort_pairs(nc.scalar.copy, t[:], bank[:])
+            nc.scalar.copy(
+                out=t[:].rearrange("a (u p e) -> a u p e", u=2, e=2),
+                in_=bank[:].rearrange("a (u e p) -> a u p e", u=2, e=2),
+            )
             dw_sorted.append(t)
 
-        q_banks = [psum.tile([P, SLOTS], F32, name="q_bank%d" % j) for j in range(LANES)]
-        for h in range(2):
-            codes = sb("dw_codes%d" % h, [P, HALF], U32)
-            scales = sb("dw_scales%d" % h, [P, HALF], U8)
-            turn_and_quantize("dw%d" % h, dw_sorted[2 * h : 2 * h + 2], codes[:], scales[:])
-            for j in range(LANES):
-                nc.tensor.matmul_mx(
-                    out=q_banks[j][:, h * HALF : (h + 1) * HALF],
-                    lhsT=pj_words[:, 2 * P * j : 2 * P * (j + 1)].bitcast(E2M1),
-                    lhsT_scale=pj_scales[:, P * j : P * (j + 1)],
-                    rhs=codes[:].bitcast(E4M3),
-                    rhs_scale=scales[:],
-                    start=True,
-                    stop=True,
-                )
+        for n in range(4):
+            first_product(n)
+
+        dw_codes = sb("dw_codes", [P, SLOTS], U32)
+        dw_scales = sb("dw_scales", [P, SLOTS], U8)
+        dw_grouped = [sb("dw%d_grouped" % h, [P, 4 * P], F32) for h in range(2)]
+        turn("dw0", dw_sorted[0:2], dw_grouped[0][:])
+        quantize(dw_codes[:, :HALF], dw_scales[:, :HALF], dw_grouped[0])
+        for c in range(2):
+            turn("dw1%d" % c, [dw_sorted[2 + c]], dw_grouped[1][:, 2 * P * c : 2 * P * (c + 1)])
+        quantize(dw_codes[:, HALF:], dw_scales[:, HALF:], dw_grouped[1])
+
+        def second_product(j, first, last, tag):
+            bank = psum.tile([P, last - first], F32, name="q_bank%d_%d" % (j, first), tag=tag)
+            nc.tensor.matmul_mx(
+                out=bank[:],
+                lhsT=pj_words[:, 2 * P * j : 2 * P * (j + 1)].bitcast(E2M1),
+                lhsT_scale=pj_scales[:, P * j : P * (j + 1)],
+                rhs=dw_codes[:, first:last].bitcast(E4M3),
+                rhs_scale=dw_scales[:, first:last],
+                start=True,
+                stop=True,
+            )
+            nc.scalar.copy(out=q_sb[j][:, first:last], in_=bank[:])
+
+        q_sb = [sb("q_sb%d" % j, [P, SLOTS], F32) for j in range(LANES)]
 
         picked = []
-        for j, after in enumerate(["x1_grouped", "m_src0", "dw1_grouped", "m_src2"]):
+        for j, after in enumerate(["x1_grouped", "m_src0", "m_src1", "dw0_grouped"]):
             t = sb("picked%d" % j, [P, SLOTS], F32, after=after)
             nc.vector.tensor_copy(t[:], m_src[j][:].indirect(offsets[:]))
             picked.append(t)
 
-        q_sb = [sb("q_sb%d" % j, [P, SLOTS], F32) for j in range(LANES)]
         decayed = []
-        for j, after in enumerate(["dw_sorted3", "dw_codes1", "m_src0", "dw1_grouped"]):
-            nc.scalar.copy(out=q_sb[j][:], in_=q_banks[j][:])
+        for j, after in enumerate(["dw_sorted3", "dw_sorted2", "x1_grouped", "m_src0"]):
+            if j == 2:
+                second_product(0, 0, HALF, "bank4")
             t = sb("decayed%d" % j, [P, SLOTS], F32, after=after)
             nc.scalar.mul(t[:], picked[j][:], DECAY)
             decayed.append(t)
+        second_product(0, HALF, SLOTS, "bank0")
+        for j in range(1, LANES):
+            second_product(j, 0, SLOTS, "bank%d" % j)
 
         def scatter(j):
-            nc.vector.tensor_tensor(m_new[j][:].indirect(offsets[:]), decayed[j][:], q_sb[j][:], ADD)
+            for first, last in ([(0, HALF), (HALF, SLOTS)] if j == 0 else [(0, SLOTS)]):
+                nc.vector.tensor_tensor(
+                    m_new[j][:].indirect(offsets[:, first // 16 : last // 16]),
+                    decayed[j][:, first:last],
+                    q_sb[j][:, first:last],
+                    ADD,
+                )
 
         WIDE = COLS // 2
-        y_grouped = [sb("y_grouped%d" % s, [P, WIDE, LANES], BF16) for s in range(2)]
+        SPLIT = 640
+        y_grouped = sb("y_grouped", [P, COLS * LANES], BF16)
+        y_lanes = y_grouped[:].rearrange("p (n t) -> p n t", t=LANES)
         y_codes = [sb("y_codes%d" % s, [P, WIDE], U32) for s in range(2)]
         y_scales = sb("y_scales", [P, COLS], U8)
 
         def hand_out(j):
             nc.sync.dma_start(out=out_rows[:, j, :], in_=m_new[j][:])
-            left, right = m_new[j][:, :WIDE], m_new[j][:, WIDE:]
+            if j < 2:
+                nc.scalar.copy(out=y_lanes[:, :, j], in_=m_new[j][:])
+                return
             if j == 2:
-                nc.scalar.copy(out=y_grouped[0][:, :, 2:4], in_=left.unsqueeze(2).to_broadcast([P, WIDE, 2]))
-            elif j == 3:
-                nc.vector.tensor_copy(out=y_grouped[0][:, :, j], in_=left)
+                nc.scalar.copy(
+                    out=y_lanes[:, :SPLIT, 2:4], in_=m_new[j][:, :SPLIT].unsqueeze(2).to_broadcast([P, SPLIT, 2])
+                )
             else:
-                nc.scalar.copy(out=y_grouped[0][:, :, j], in_=left)
-            nc.scalar.copy(out=y_grouped[1][:, :, j], in_=right)
+                nc.vector.tensor_copy(out=y_lanes[:, :WIDE, j], in_=m_new[j][:, :WIDE])
+                nc.vector.tensor_copy(out=y_lanes[:, WIDE:SPLIT, j], in_=m_new[j][:, WIDE:SPLIT])
+            nc.scalar.copy(out=y_lanes[:, SPLIT:, j], in_=m_new[j][:, SPLIT:])
 
         for j in range(LANES):
             scatter(j)
             hand_out(j)
 
         words_out = out_1[0].rearrange("p n t -> p (n t)").bitcast(I32)
+
+        def store_scales(queue, q):
+            queue.dma_start(
+                out=out_2[0, 4 * q : 4 * q + 4, :].bitcast(I32),
+                in_=y_scales[32 * q : 32 * q + 4, :].bitcast(I32),
+            )
+
         for s in range(2):
             cols = slice(s * WIDE, (s + 1) * WIDE)
             nc.vector.quantize_mx(
                 out=y_codes[s][:].bitcast(E4M3),
                 scales=y_scales[:, cols],
-                in_=y_grouped[s][:].rearrange("p n t -> p (n t)"),
+                in_=y_grouped[:, s * WIDE * LANES : (s + 1) * WIDE * LANES],
             )
+            if s == 1:
+                store_scales(nc.sync, 0)
             nc.sync.dma_start(out=words_out[:, cols], in_=y_codes[s][:].bitcast(I32))
-        for q in range(4):
-            queue = nc.sync if q % 2 == 0 else nc.scalar
-            queue.dma_start(
-                out=out_2[0, 4 * q : 4 * q + 4, :].bitcast(I32),
-                in_=y_scales[32 * q : 32 * q + 4, :].bitcast(I32),
-            )
+        for q in range(1, 4):
+            store_scales(nc.scalar, q)

@@ -37,9 +37,7 @@ def tile_attend_glowmom_pl_kernel(
 
         offsets = keep.tile([P, SLOTS // 16], U16, name="offsets")
         ident = sb("ident", [P, P], F32)
-        x_head = sb("x_head", [P, 2, R], F32)
-        x_tail = [sb("x_tail%d" % c, [P, R], F32) for c in range(2)]
-        x_raw = [x_head[:, 0, :], x_head[:, 1, :], x_tail[0][:], x_tail[1][:]]
+        x_raw = [sb("x_raw%d" % h, [P, 2, R], F32) for h in range(2)]
         g_raw = [sb("g_raw%d" % h, [P, LANES, HALF], F32) for h in range(2)]
         pj_raw = sb("pj_raw", [P, 2 * K], U8)
         pjs_raw = sb("pjs_raw", [P, K], U8)
@@ -54,15 +52,14 @@ def tile_attend_glowmom_pl_kernel(
         nc.gpsimd.memset(pjs_raw[:].bitcast(I32), 0)
         make_identity(nc, ident[:])
 
-        nc.sync.dma_start(out=x_head[:], in_=x_rows[:, 0:2, :])
-        for c in range(2):
-            nc.sync.dma_start(out=x_tail[c][:], in_=x_rows[:, 2 + c, :])
-        nc.sync.dma_start(out=pj_raw[:].bitcast(I32), in_=Pj_words[0].bitcast(I32))
+        nc.sync.dma_start(out=x_raw[0][:], in_=x_rows[:, 0:2, :])
         for q in range(4):
-            nc.scalar.dma_start(
+            nc.sync.dma_start(
                 out=pjs_raw[32 * q : 32 * q + 4, :].bitcast(I32),
                 in_=Pj_scales[0, 4 * q : 4 * q + 4, :].bitcast(I32),
             )
+        nc.sync.dma_start(out=x_raw[1][:], in_=x_rows[:, 2:4, :])
+        nc.sync.dma_start(out=pj_raw[:].bitcast(I32), in_=Pj_words[0].bitcast(I32))
         for h in range(2):
             nc.sync.dma_start(out=g_raw[h][:], in_=g_rows[:, :, h * HALF : (h + 1) * HALF])
         nc.sync.dma_start(offsets[:], offs)
@@ -99,7 +96,7 @@ def tile_attend_glowmom_pl_kernel(
             grouped = sb("x%d_grouped" % h, [P, 4 * P], F32)
             for c in range(2):
                 t = sb("x_sorted%d%d" % (h, c), [P, R], BF16)
-                sort_pairs(nc.vector.tensor_copy if h + c else nc.scalar.copy, t[:], x_raw[2 * h + c])
+                sort_pairs((nc.scalar.copy, nc.vector.tensor_copy)[c], t[:], x_raw[h][:, c, :])
                 turn("x%d%d" % (h, c), [t], grouped[:, 2 * P * c : 2 * P * (c + 1)])
             cols = slice(h * 2 * P, (h + 1) * 2 * P)
             quantize(x_codes[:, cols], x_scales[:, cols], grouped)
@@ -184,13 +181,13 @@ def tile_attend_glowmom_pl_kernel(
         q_sb = [sb("q_sb%d" % j, [P, SLOTS], F32) for j in range(LANES)]
 
         picked = []
-        for j, after in enumerate(["x1_grouped", "m_src0", "m_src1", "dw0_grouped"]):
+        for j, after in enumerate(["g_raw1", "x1_grouped", "m_src0", "dw0_grouped"]):
             t = sb("picked%d" % j, [P, SLOTS], F32, after=after)
             nc.vector.tensor_copy(t[:], m_src[j][:].indirect(offsets[:]))
             picked.append(t)
 
         decayed = []
-        for j, after in enumerate(["dw_sorted3", "dw_sorted2", "x1_grouped", "m_src0"]):
+        for j, after in enumerate(["dw_sorted3", "dw_sorted2", "g_raw1", "x1_grouped"]):
             if j == 2:
                 second_product(0, 0, HALF, "bank4")
             t = sb("decayed%d" % j, [P, SLOTS], F32, after=after)

@@ -72,7 +72,7 @@ def tile_attend_glowmom_pl_kernel(
             n = len(sorted_tiles)
             bank = psum.tile([P, n, 2, P], F32, name=name + "_bank", tag="turn", bufs=3)
             for c in range(n):
-                words = sorted_tiles[c][:].bitcast(F32)
+                words = sorted_tiles[c].bitcast(F32)
                 for u in range(2):
                     nc.tensor.transpose(bank[:, c, u, :], words[:, u * P : (u + 1) * P], ident[:])
             nc.scalar.copy(
@@ -92,45 +92,71 @@ def tile_attend_glowmom_pl_kernel(
         x_codes = sb("x_codes", [P, D], U32)
         x_scales = sb("x_scales", [P, D], U8)
 
-        def quantize_x(h):
-            grouped = sb("x%d_grouped" % h, [P, 4 * P], F32)
+        x_grouped = [sb("x%d_grouped" % h, [P, 4 * P], F32) for h in range(2)]
+
+        def turn_x(h):
             for c in range(2):
                 t = sb("x_sorted%d%d" % (h, c), [P, R], BF16)
-                sort_pairs((nc.scalar.copy, nc.vector.tensor_copy)[c], t[:], x_raw[h][:, c, :])
-                turn("x%d%d" % (h, c), [t], grouped[:, 2 * P * c : 2 * P * (c + 1)])
-            cols = slice(h * 2 * P, (h + 1) * 2 * P)
-            quantize(x_codes[:, cols], x_scales[:, cols], grouped)
+                sort_pairs(nc.vector.tensor_copy, t[:], x_raw[h][:, c, :])
+                turn("x%d%d" % (h, c), [t[:]], x_grouped[h][:, 2 * P * c : 2 * P * (c + 1)])
 
-        quantize_x(0)
-        quantize_x(1)
+        def quantize_x(h):
+            cols = slice(h * 2 * P, (h + 1) * 2 * P)
+            quantize(x_codes[:, cols], x_scales[:, cols], x_grouped[h])
+
+        picked = [None] * LANES
+        decayed = [None] * LANES
+
+        def gather(j, after):
+            picked[j] = sb("picked%d" % j, [P, SLOTS], F32, after=after)
+            nc.vector.tensor_copy(picked[j][:], m_src[j][:].indirect(offsets[:]))
+
+        def decay(j, after):
+            decayed[j] = sb("decayed%d" % j, [P, SLOTS], F32, after=after)
+            nc.scalar.mul(decayed[j][:], picked[j][:], DECAY)
+
+        turn_x(0)
         pj_words = sb("pj_words", [P, 2 * K], U8)
         pj_scales = sb("pj_scales", [P, K], U8)
-        nc.vector.tensor_copy(
-            out=pj_words[:].bitcast(U16).rearrange("p (j m) -> p j m", j=LANES),
-            in_=pj_raw[:].bitcast(U16).rearrange("p (m j) -> p j m", j=LANES),
-        )
         nc.vector.tensor_copy(
             out=pj_scales[:].rearrange("p (j m) -> p j m", j=LANES),
             in_=pjs_raw[:].rearrange("p (m j) -> p j m", j=LANES),
         )
+        turn_x(1)
+        quantize_x(0)
+        nc.vector.tensor_copy(
+            out=pj_words[:].bitcast(U16).rearrange("p (j m) -> p j m", j=LANES),
+            in_=pj_raw[:].bitcast(U16).rearrange("p (m j) -> p j m", j=LANES),
+        )
 
         g_codes = [sb("g_codes%d" % h, [P, HALF], U32) for h in range(2)]
         g_scales = [sb("g_scales%d" % h, [P, HALF], U8) for h in range(2)]
-        for h in range(2):
-            grouped = sb("g_grouped%d" % h, [P, HALF * LANES], BF16, after="x%d_grouped" % h)
+
+        def group_g(h, share):
+            grouped = sb("g_grouped%d" % h, [P, HALF * LANES], BF16, after=("x0_grouped", "x1_grouped")[h])
             dst = grouped[:].rearrange("p (c i t) -> p c t i", i=4, t=LANES)
             src = g_raw[h][:].rearrange("p t (c i) -> p c t i", i=4)
-            if h == 0:
-                nc.vector.tensor_copy(out=dst[:, :32], in_=src[:, :32])
-                nc.scalar.copy(out=dst[:, 32:], in_=src[:, 32:])
-            else:
-                nc.vector.tensor_copy(out=dst, in_=src)
-            for first, last in ([(0, P), (P, HALF)] if h == 0 else [(0, HALF)]):
+            nc.vector.tensor_copy(out=dst[:, :share], in_=src[:, :share])
+            if share < HALF // 4:
+                nc.scalar.copy(out=dst[:, share:], in_=src[:, share:])
+            return grouped
+
+        def quantize_g(h, grouped, pieces):
+            for first, last in pieces:
                 nc.vector.quantize_mx(
                     out=g_codes[h][:, first:last].bitcast(E5M2),
                     scales=g_scales[h][:, first:last],
                     in_=grouped[:, LANES * first : LANES * last],
                 )
+
+        grouped0 = group_g(0, 64)
+        quantize_x(1)
+        quantize_g(0, grouped0, [(0, HALF)])
+        grouped1 = group_g(1, 32)
+        quantize_g(1, grouped1, [(P, HALF), (0, P)])
+        gather(0, "g_raw1")
+        gather(1, "x1_grouped")
+        gather(2, "m_src0")
 
         dw_sorted = []
 
@@ -146,24 +172,28 @@ def tile_attend_glowmom_pl_kernel(
                 start=True,
                 stop=True,
             )
+            return bank
+
+        def round_dw(n):
+            bank = dw_banks[n]
             t = sb("dw_sorted%d" % n, [P, D], BF16)
             nc.scalar.copy(
                 out=t[:].rearrange("a (u p e) -> a u p e", u=2, e=2),
                 in_=bank[:].rearrange("a (u e p) -> a u p e", u=2, e=2),
             )
-            dw_sorted.append(t)
-
-        for n in range(4):
-            first_product(n)
+            dw_sorted.append(t[:])
 
         dw_codes = sb("dw_codes", [P, SLOTS], U32)
         dw_scales = sb("dw_scales", [P, SLOTS], U8)
-        dw_grouped = [sb("dw%d_grouped" % h, [P, 4 * P], F32) for h in range(2)]
-        turn("dw0", dw_sorted[0:2], dw_grouped[0][:])
-        quantize(dw_codes[:, :HALF], dw_scales[:, :HALF], dw_grouped[0])
-        for c in range(2):
-            turn("dw1%d" % c, [dw_sorted[2 + c]], dw_grouped[1][:, 2 * P * c : 2 * P * (c + 1)])
-        quantize(dw_codes[:, HALF:], dw_scales[:, HALF:], dw_grouped[1])
+        dw_grouped = [sb("dw%d_grouped" % h, [P, 4 * P], F32, after=("g_codes1", None)[h]) for h in range(2)]
+        dw_banks = [first_product(n) for n in range(4)]
+        for n in range(4):
+            round_dw(n)
+        for h in range(2):
+            turn("dw%d" % h, dw_sorted[2 * h : 2 * h + 2], dw_grouped[h][:])
+            cols = slice(h * HALF, (h + 1) * HALF)
+            quantize(dw_codes[:, cols], dw_scales[:, cols], dw_grouped[h])
+        gather(3, "g_codes1")
 
         def second_product(j, first, last, tag):
             bank = psum.tile([P, last - first], F32, name="q_bank%d_%d" % (j, first), tag=tag)
@@ -180,21 +210,11 @@ def tile_attend_glowmom_pl_kernel(
 
         q_sb = [sb("q_sb%d" % j, [P, SLOTS], F32) for j in range(LANES)]
 
-        picked = []
-        for j, after in enumerate(["g_raw1", "x1_grouped", "m_src0", "dw0_grouped"]):
-            t = sb("picked%d" % j, [P, SLOTS], F32, after=after)
-            nc.vector.tensor_copy(t[:], m_src[j][:].indirect(offsets[:]))
-            picked.append(t)
-
-        decayed = []
-        for j, after in enumerate(["dw_sorted3", "dw_sorted2", "g_raw1", "x1_grouped"]):
-            if j == 2:
-                second_product(0, 0, HALF, "bank4")
-            t = sb("decayed%d" % j, [P, SLOTS], F32, after=after)
-            nc.scalar.mul(t[:], picked[j][:], DECAY)
-            decayed.append(t)
+        decay(0, "dw_sorted3")
+        second_product(0, 0, HALF, "bank4")
         second_product(0, HALF, SLOTS, "bank0")
-        for j in range(1, LANES):
+        for j, after in ((1, "dw1_grouped"), (2, "g_raw1"), (3, "x1_grouped")):
+            decay(j, after)
             second_product(j, 0, SLOTS, "bank%d" % j)
 
         def scatter(j):

@@ -38,7 +38,7 @@ def tile_attend_glowmom_pl_kernel(
         offsets = keep.tile([P, SLOTS // 16], U16, name="offsets")
         ident = sb("ident", [P, P], F32)
         x_raw = [sb("x_raw%d" % h, [P, 2, R], F32) for h in range(2)]
-        g_raw = [sb("g_raw%d" % h, [P, LANES, HALF], F32) for h in range(2)]
+        g_raw = [sb("g_raw%d" % u, [P, 2, SLOTS], F32) for u in range(2)]
         pj_raw = sb("pj_raw", [P, 2 * K], U8)
         pjs_raw = sb("pjs_raw", [P, K], U8)
         m_src = [sb("m_src%d" % j, [P, COLS], F32) for j in range(LANES)]
@@ -60,8 +60,8 @@ def tile_attend_glowmom_pl_kernel(
             )
         nc.sync.dma_start(out=x_raw[1][:], in_=x_rows[:, 2:4, :])
         nc.sync.dma_start(out=pj_raw[:].bitcast(I32), in_=Pj_words[0].bitcast(I32))
-        for h in range(2):
-            nc.sync.dma_start(out=g_raw[h][:], in_=g_rows[:, :, h * HALF : (h + 1) * HALF])
+        for u in range(2):
+            nc.sync.dma_start(out=g_raw[u][:], in_=g_rows[:, 2 * u : 2 * u + 2, :])
         nc.sync.dma_start(offsets[:], offs)
         for j in range(LANES):
             nc.sync.dma_start(out=m_src[j][:], in_=m_rows[:, j, :])
@@ -132,30 +132,30 @@ def tile_attend_glowmom_pl_kernel(
         g_codes = [sb("g_codes%d" % h, [P, HALF], U32) for h in range(2)]
         g_scales = [sb("g_scales%d" % h, [P, HALF], U8) for h in range(2)]
 
-        def group_g(h, share):
-            grouped = sb("g_grouped%d" % h, [P, HALF * LANES], BF16, after=("x0_grouped", "x1_grouped")[h])
-            dst = grouped[:].rearrange("p (c i t) -> p c t i", i=4, t=LANES)
-            src = g_raw[h][:].rearrange("p t (c i) -> p c t i", i=4)
-            nc.vector.tensor_copy(out=dst[:, :share], in_=src[:, :share])
-            if share < HALF // 4:
-                nc.scalar.copy(out=dst[:, share:], in_=src[:, share:])
-            return grouped
+        g_grouped = sb("g_grouped", [P, SLOTS * LANES], BF16, after="x0_grouped")
+        g_pairs = g_grouped[:].rearrange("p (i u e) -> p u i e", u=2, e=2)
 
-        def quantize_g(h, grouped, pieces):
-            for first, last in pieces:
-                nc.vector.quantize_mx(
-                    out=g_codes[h][:, first:last].bitcast(E5M2),
-                    scales=g_scales[h][:, first:last],
-                    in_=grouped[:, LANES * first : LANES * last],
-                )
+        def group_g(copy, u, first, last):
+            copy(out=g_pairs[:, u, first:last, :], in_=g_raw[u][:, :, first:last].rearrange("p e i -> p i e"))
 
-        grouped0 = group_g(0, 64)
+        def quantize_g(first, last):
+            h, cols = first // HALF, slice(first % HALF, first % HALF + last - first)
+            nc.vector.quantize_mx(
+                out=g_codes[h][:, cols].bitcast(E5M2),
+                scales=g_scales[h][:, cols],
+                in_=g_grouped[:, LANES * first : LANES * last],
+            )
+
+        group_g(nc.vector.tensor_copy, 0, 0, SLOTS)
         quantize_x(1)
-        quantize_g(0, grouped0, [(0, HALF)])
-        grouped1 = group_g(1, 32)
-        quantize_g(1, grouped1, [(P, HALF), (0, P)])
+        group_g(nc.scalar.copy, 1, 0, P)
+        group_g(nc.vector.tensor_copy, 1, P, 3 * P)
+        group_g(nc.scalar.copy, 1, 3 * P, SLOTS)
+        quantize_g(0, P)
+        quantize_g(P, HALF)
+        quantize_g(HALF, SLOTS)
         gather(0, "g_raw1")
-        gather(1, "x1_grouped")
+        gather(1, "x0_grouped")
         gather(2, "m_src0")
 
         dw_sorted = []
@@ -183,17 +183,17 @@ def tile_attend_glowmom_pl_kernel(
             )
             dw_sorted.append(t[:])
 
-        dw_codes = sb("dw_codes", [P, SLOTS], U32)
-        dw_scales = sb("dw_scales", [P, SLOTS], U8)
-        dw_grouped = [sb("dw%d_grouped" % h, [P, 4 * P], F32, after=("g_codes1", None)[h]) for h in range(2)]
         dw_banks = [first_product(n) for n in range(4)]
         for n in range(4):
             round_dw(n)
-        for h in range(2):
-            turn("dw%d" % h, dw_sorted[2 * h : 2 * h + 2], dw_grouped[h][:])
-            cols = slice(h * HALF, (h + 1) * HALF)
-            quantize(dw_codes[:, cols], dw_scales[:, cols], dw_grouped[h])
-        gather(3, "g_codes1")
+        dw_codes = sb("dw_codes", [P, SLOTS], U32, after="dw_sorted3")
+        dw_scales = sb("dw_scales", [P, SLOTS], U8)
+        for first, last, after in ((0, 2, "g_codes1"), (2, 3, None), (3, 4, None)):
+            grouped = sb("dw%d_grouped" % first, [P, 2 * P * (last - first)], F32, after=after)
+            turn("dw%d" % first, dw_sorted[first:last], grouped[:])
+            cols = slice(first * P, last * P)
+            quantize(dw_codes[:, cols], dw_scales[:, cols], grouped)
+        gather(3, "dw2_grouped")
 
         def second_product(j, first, last, tag):
             bank = psum.tile([P, last - first], F32, name="q_bank%d_%d" % (j, first), tag=tag)
@@ -210,11 +210,14 @@ def tile_attend_glowmom_pl_kernel(
 
         q_sb = [sb("q_sb%d" % j, [P, SLOTS], F32) for j in range(LANES)]
 
-        decay(0, "dw_sorted3")
+        decay(0, "dw_sorted2")
+        decay(1, "g_raw1")
         second_product(0, 0, HALF, "bank4")
         second_product(0, HALF, SLOTS, "bank0")
-        for j, after in ((1, "dw1_grouped"), (2, "g_raw1"), (3, "x1_grouped")):
-            decay(j, after)
+        decay(2, "x0_grouped")
+        second_product(1, 0, SLOTS, "bank1")
+        decay(3, "m_src0")
+        for j in range(2, LANES):
             second_product(j, 0, SLOTS, "bank%d" % j)
 
         def scatter(j):

@@ -63,7 +63,7 @@ def tile_attend_glowmom_pl_kernel(
         for u in range(2):
             nc.sync.dma_start(out=g_raw[u][:], in_=g_rows[:, 2 * u : 2 * u + 2, :])
         nc.sync.dma_start(offsets[:], offs)
-        for j in range(LANES):
+        for j in (0, 2, 3, 1):
             nc.sync.dma_start(out=m_src[j][:], in_=m_rows[:, j, :])
         for j in range(LANES):
             nc.sync.dma_start(out=m_new[j][:], in_=m_rows[:, j, :])
@@ -107,21 +107,24 @@ def tile_attend_glowmom_pl_kernel(
         picked = [None] * LANES
         decayed = [None] * LANES
 
-        def gather(j, after):
-            picked[j] = sb("picked%d" % j, [P, SLOTS], F32, after=after)
-            nc.vector.tensor_copy(picked[j][:], m_src[j][:].indirect(offsets[:]))
+        def gather(lanes, after):
+            t = sb("picked%d" % lanes[0], [P, len(lanes), SLOTS], F32, after=after)
+            for n, j in enumerate(lanes):
+                nc.vector.tensor_copy(t[:, n, :], m_src[j][:].indirect(offsets[:]))
+            picked[lanes[0]] = t
 
-        def decay(j, after):
-            decayed[j] = sb("decayed%d" % j, [P, SLOTS], F32, after=after)
-            nc.scalar.mul(decayed[j][:], picked[j][:], DECAY)
+        def decay(lanes, after):
+            t = sb("decayed%d" % lanes[0], [P, len(lanes), SLOTS], F32, after=after)
+            nc.scalar.mul(t[:], picked[lanes[0]][:], DECAY)
+            for n, j in enumerate(lanes):
+                decayed[j] = t[:, n, :]
 
         turn_x(0)
         pj_words = sb("pj_words", [P, 2 * K], U8)
-        pj_scales = sb("pj_scales", [P, K], U8)
-        nc.vector.tensor_copy(
-            out=pj_scales[:].rearrange("p (j m) -> p j m", j=LANES),
-            in_=pjs_raw[:].rearrange("p (m j) -> p j m", j=LANES),
-        )
+        pj_scales = [sb("pj_scales0", [P, P], U8), sb("pj_scales1", [P, K - P], U8)]
+        pjs_lanes = pjs_raw[:].rearrange("p (m j) -> p j m", j=LANES)
+        nc.vector.tensor_copy(out=pj_scales[0][:], in_=pjs_lanes[:, 0, :])
+        nc.vector.tensor_copy(out=pj_scales[1][:].rearrange("p (j m) -> p j m", m=P), in_=pjs_lanes[:, 1:, :])
         turn_x(1)
         quantize_x(0)
         nc.vector.tensor_copy(
@@ -154,9 +157,8 @@ def tile_attend_glowmom_pl_kernel(
         quantize_g(0, P)
         quantize_g(P, HALF)
         quantize_g(HALF, SLOTS)
-        gather(0, "g_raw1")
-        gather(1, "x0_grouped")
-        gather(2, "m_src0")
+        gather((0,), "g_raw1")
+        gather((2, 3), "x0_grouped")
 
         dw_sorted = []
 
@@ -193,14 +195,14 @@ def tile_attend_glowmom_pl_kernel(
             turn("dw%d" % first, dw_sorted[first:last], grouped[:])
             cols = slice(first * P, last * P)
             quantize(dw_codes[:, cols], dw_scales[:, cols], grouped)
-        gather(3, "dw2_grouped")
+        gather((1,), "dw2_grouped")
 
         def second_product(j, first, last, tag):
             bank = psum.tile([P, last - first], F32, name="q_bank%d_%d" % (j, first), tag=tag)
             nc.tensor.matmul_mx(
                 out=bank[:],
                 lhsT=pj_words[:, 2 * P * j : 2 * P * (j + 1)].bitcast(E2M1),
-                lhsT_scale=pj_scales[:, P * j : P * (j + 1)],
+                lhsT_scale=pj_scales[0][:] if j == 0 else pj_scales[1][:, P * (j - 1) : P * j],
                 rhs=dw_codes[:, first:last].bitcast(E4M3),
                 rhs_scale=dw_scales[:, first:last],
                 start=True,
@@ -210,49 +212,40 @@ def tile_attend_glowmom_pl_kernel(
 
         q_sb = [sb("q_sb%d" % j, [P, SLOTS], F32) for j in range(LANES)]
 
-        decay(0, "dw_sorted2")
-        decay(1, "g_raw1")
+        decay((0,), "dw_sorted2")
         second_product(0, 0, HALF, "bank4")
-        second_product(0, HALF, SLOTS, "bank0")
-        decay(2, "x0_grouped")
-        second_product(1, 0, SLOTS, "bank1")
-        decay(3, "m_src0")
-        for j in range(2, LANES):
-            second_product(j, 0, SLOTS, "bank%d" % j)
+        second_product(0, HALF, 3 * P, "bank0")
+        second_product(0, 3 * P, SLOTS, "bank1")
+        second_product(1, 0, SLOTS, "bank2")
+        decay((1,), "pj_scales0")
+        second_product(2, 0, SLOTS, "bank3")
+        second_product(3, 0, SLOTS, "bank4")
+        decay((2, 3), "pj_scales1")
 
         def scatter(j):
-            for first, last in ([(0, HALF), (HALF, SLOTS)] if j == 0 else [(0, SLOTS)]):
-                nc.vector.tensor_tensor(
-                    m_new[j][:].indirect(offsets[:, first // 16 : last // 16]),
-                    decayed[j][:, first:last],
-                    q_sb[j][:, first:last],
-                    ADD,
-                )
+            nc.vector.tensor_tensor(m_new[j][:].indirect(offsets[:]), decayed[j], q_sb[j][:], ADD)
 
         WIDE = COLS // 2
-        SPLIT = 640
+        QUARTER = COLS // 4
+        SPLIT = 416
         y_grouped = sb("y_grouped", [P, COLS * LANES], BF16)
         y_lanes = y_grouped[:].rearrange("p (n t) -> p n t", t=LANES)
         y_codes = [sb("y_codes%d" % s, [P, WIDE], U32) for s in range(2)]
         y_scales = sb("y_scales", [P, COLS], U8)
 
-        def hand_out(j):
-            nc.sync.dma_start(out=out_rows[:, j, :], in_=m_new[j][:])
-            if j < 2:
-                nc.scalar.copy(out=y_lanes[:, :, j], in_=m_new[j][:])
-                return
-            if j == 2:
-                nc.scalar.copy(
-                    out=y_lanes[:, :SPLIT, 2:4], in_=m_new[j][:, :SPLIT].unsqueeze(2).to_broadcast([P, SPLIT, 2])
-                )
-            else:
-                nc.vector.tensor_copy(out=y_lanes[:, :WIDE, j], in_=m_new[j][:, :WIDE])
-                nc.vector.tensor_copy(out=y_lanes[:, WIDE:SPLIT, j], in_=m_new[j][:, WIDE:SPLIT])
-            nc.scalar.copy(out=y_lanes[:, SPLIT:, j], in_=m_new[j][:, SPLIT:])
+        def round_lane(copy, j, first, last):
+            copy(out=y_lanes[:, first:last, j], in_=m_new[j][:, first:last])
 
         for j in range(LANES):
             scatter(j)
-            hand_out(j)
+            nc.sync.dma_start(out=out_rows[:, j, :], in_=m_new[j][:])
+            if j < 3:
+                round_lane(nc.scalar.copy, j, 0 if j < 2 else SPLIT, COLS)
+        for first, last in ((SPLIT, WIDE), (WIDE, 3 * QUARTER), (3 * QUARTER, COLS)):
+            round_lane(nc.scalar.copy, 3, first, last)
+        round_lane(nc.vector.tensor_copy, 2, 0, SPLIT)
+        round_lane(nc.vector.tensor_copy, 3, 0, QUARTER)
+        round_lane(nc.vector.tensor_copy, 3, QUARTER, SPLIT)
 
         words_out = out_1[0].rearrange("p n t -> p (n t)").bitcast(I32)
 
@@ -264,11 +257,13 @@ def tile_attend_glowmom_pl_kernel(
 
         for s in range(2):
             cols = slice(s * WIDE, (s + 1) * WIDE)
-            nc.vector.quantize_mx(
-                out=y_codes[s][:].bitcast(E4M3),
-                scales=y_scales[:, cols],
-                in_=y_grouped[:, s * WIDE * LANES : (s + 1) * WIDE * LANES],
-            )
+            for first in (s * WIDE, s * WIDE + QUARTER):
+                last = first + QUARTER
+                nc.vector.quantize_mx(
+                    out=y_codes[s][:, first - s * WIDE : last - s * WIDE].bitcast(E4M3),
+                    scales=y_scales[:, first:last],
+                    in_=y_grouped[:, first * LANES : last * LANES],
+                )
             if s == 1:
                 store_scales(nc.sync, 0)
             nc.sync.dma_start(out=words_out[:, cols], in_=y_codes[s][:].bitcast(I32))

@@ -230,7 +230,7 @@ def tile_attend_glowmom_pl_kernel(
         SPLIT = 416
         y_grouped = sb("y_grouped", [P, COLS * LANES], BF16)
         y_lanes = y_grouped[:].rearrange("p (n t) -> p n t", t=LANES)
-        y_codes = [sb("y_codes%d" % s, [P, WIDE], U32) for s in range(2)]
+        y_codes = [sb("y_codes%d" % s, [P, QUARTER], U32) for s in range(4)]
         y_scales = sb("y_scales", [P, COLS], U8)
 
         def round_lane(copy, j, first, last):
@@ -255,17 +255,13 @@ def tile_attend_glowmom_pl_kernel(
                 in_=y_scales[32 * q : 32 * q + 4, :].bitcast(I32),
             )
 
-        for s in range(2):
-            cols = slice(s * WIDE, (s + 1) * WIDE)
-            for first in (s * WIDE, s * WIDE + QUARTER):
-                last = first + QUARTER
-                nc.vector.quantize_mx(
-                    out=y_codes[s][:, first - s * WIDE : last - s * WIDE].bitcast(E4M3),
-                    scales=y_scales[:, first:last],
-                    in_=y_grouped[:, first * LANES : last * LANES],
-                )
-            if s == 1:
-                store_scales(nc.sync, 0)
+        for s in range(4):
+            cols = slice(s * QUARTER, (s + 1) * QUARTER)
+            nc.vector.quantize_mx(
+                out=y_codes[s][:].bitcast(E4M3),
+                scales=y_scales[:, cols],
+                in_=y_grouped[:, s * QUARTER * LANES : (s + 1) * QUARTER * LANES],
+            )
             nc.sync.dma_start(out=words_out[:, cols], in_=y_codes[s][:].bitcast(I32))
-        for q in range(1, 4):
-            store_scales(nc.scalar, q)
+        for q in range(4):
+            store_scales((nc.scalar, nc.sync)[q % 2], q)

@@ -21,6 +21,10 @@ D = R = K = SLOTS = 512
 COLS = 1024
 HALF = SLOTS // 2
 DECAY = 0.9
+ORDER = (0, 2, 3, 1)
+LATE = 64
+G_SPLIT = 320
+SPLIT = 576
 FLOPS = 2 * D * R * SLOTS + 2 * K * D * SLOTS
 
 
@@ -30,11 +34,15 @@ def tile_attend_glowmom_pl_kernel(
     nc = tc.nc
     with ExitStack() as ctx:
         keep = ctx.enter_context(tc.tile_pool(name="keep", bufs=1))
+        shared = ctx.enter_context(tc.tile_pool(name="shared", bufs=1))
         psum = ctx.enter_context(tc.psum_pool(name="psum", bufs=1))
 
         def sb(name, shape, dtype, after=None):
+            if isinstance(after, int):
+                return shared.tile(shape, dtype, name=name, offset=after, align_bytes=64)
             return keep.tile(shape, dtype, name=name, tag=after or name, align_bytes=64)
 
+        first, second, third, last = ORDER
         offsets = keep.tile([P, SLOTS // 16], U16, name="offsets")
         ident = sb("ident", [P, P], F32)
         x_raw = [sb("x_raw%d" % h, [P, 2, R], F32) for h in range(2)]
@@ -63,9 +71,9 @@ def tile_attend_glowmom_pl_kernel(
         for u in range(2):
             nc.sync.dma_start(out=g_raw[u][:], in_=g_rows[:, 2 * u : 2 * u + 2, :])
         nc.sync.dma_start(offsets[:], offs)
-        for j in (0, 2, 3, 1):
+        for j in (first, third, last, second):
             nc.sync.dma_start(out=m_src[j][:], in_=m_rows[:, j, :])
-        for j in range(LANES):
+        for j in ORDER:
             nc.sync.dma_start(out=m_new[j][:], in_=m_rows[:, j, :])
 
         def turn(name, sorted_tiles, words_out):
@@ -92,7 +100,7 @@ def tile_attend_glowmom_pl_kernel(
         x_codes = sb("x_codes", [P, D], U32)
         x_scales = sb("x_scales", [P, D], U8)
 
-        x_grouped = [sb("x%d_grouped" % h, [P, 4 * P], F32) for h in range(2)]
+        x_grouped = [sb("x0_grouped", [P, 4 * P], F32, after=3072), sb("x1_grouped", [P, 4 * P], F32)]
 
         def turn_x(h):
             for c in range(2):
@@ -113,11 +121,14 @@ def tile_attend_glowmom_pl_kernel(
                 nc.vector.tensor_copy(t[:, n, :], m_src[j][:].indirect(offsets[:]))
             picked[lanes[0]] = t
 
-        def decay(lanes, after):
-            t = sb("decayed%d" % lanes[0], [P, len(lanes), SLOTS], F32, after=after)
-            nc.scalar.mul(t[:], picked[lanes[0]][:], DECAY)
+        def decay(lanes, after, held_back=0):
+            t = sb("decayed%d" % lanes[0], [P, len(lanes) * SLOTS], F32, after=after)
+            src = picked[lanes[0]][:].rearrange("p n i -> p (n i)")
+            cut = len(lanes) * SLOTS - held_back
+            nc.scalar.mul(t[:, :cut], src[:, :cut], DECAY)
             for n, j in enumerate(lanes):
-                decayed[j] = t[:, n, :]
+                decayed[j] = t[:, n * SLOTS : (n + 1) * SLOTS]
+            return t[:, cut:], src[:, cut:]
 
         turn_x(0)
         pj_words = sb("pj_words", [P, 2 * K], U8)
@@ -135,30 +146,33 @@ def tile_attend_glowmom_pl_kernel(
         g_codes = [sb("g_codes%d" % h, [P, HALF], U32) for h in range(2)]
         g_scales = [sb("g_scales%d" % h, [P, HALF], U8) for h in range(2)]
 
-        g_grouped = sb("g_grouped", [P, SLOTS * LANES], BF16, after="x0_grouped")
-        g_pairs = g_grouped[:].rearrange("p (i u e) -> p u i e", u=2, e=2)
+        g_grouped = [sb("g_grouped%d" % h, [P, HALF * LANES], BF16, after=2048 * (h + 1)) for h in range(2)]
 
-        def group_g(copy, u, first, last):
-            copy(out=g_pairs[:, u, first:last, :], in_=g_raw[u][:, :, first:last].rearrange("p e i -> p i e"))
+        def group_g(copy, u, lo, hi):
+            h, cols = lo // HALF, slice(lo % HALF, lo % HALF + hi - lo)
+            pairs = g_grouped[h][:].rearrange("p (i u e) -> p u i e", u=2, e=2)
+            copy(out=pairs[:, u, cols, :], in_=g_raw[u][:, :, lo:hi].rearrange("p e i -> p i e"))
 
-        def quantize_g(first, last):
-            h, cols = first // HALF, slice(first % HALF, first % HALF + last - first)
+        def quantize_g(lo, hi):
+            h, cols = lo // HALF, slice(lo % HALF, lo % HALF + hi - lo)
             nc.vector.quantize_mx(
                 out=g_codes[h][:, cols].bitcast(E5M2),
                 scales=g_scales[h][:, cols],
-                in_=g_grouped[:, LANES * first : LANES * last],
+                in_=g_grouped[h][:, LANES * cols.start : LANES * cols.stop],
             )
 
-        group_g(nc.vector.tensor_copy, 0, 0, SLOTS)
+        group_g(nc.vector.tensor_copy, 0, 0, HALF)
+        group_g(nc.vector.tensor_copy, 0, HALF, SLOTS)
         quantize_x(1)
-        group_g(nc.scalar.copy, 1, 0, P)
-        group_g(nc.vector.tensor_copy, 1, P, 3 * P)
-        group_g(nc.scalar.copy, 1, 3 * P, SLOTS)
+        group_g(nc.scalar.copy, 1, G_SPLIT, SLOTS)
+        group_g(nc.vector.tensor_copy, 1, 0, P)
+        group_g(nc.vector.tensor_copy, 1, P, HALF)
+        group_g(nc.vector.tensor_copy, 1, HALF, G_SPLIT)
         quantize_g(0, P)
         quantize_g(P, HALF)
         quantize_g(HALF, SLOTS)
-        gather((0,), "g_raw1")
-        gather((2, 3), "x0_grouped")
+        gather((first,), 1024)
+        gather((third, last), 4096)
 
         dw_sorted = []
 
@@ -188,64 +202,60 @@ def tile_attend_glowmom_pl_kernel(
         dw_banks = [first_product(n) for n in range(4)]
         for n in range(4):
             round_dw(n)
-        dw_codes = sb("dw_codes", [P, SLOTS], U32, after="dw_sorted3")
+        dw_codes = sb("dw_codes", [P, SLOTS], U32)
         dw_scales = sb("dw_scales", [P, SLOTS], U8)
-        for first, last, after in ((0, 2, "g_codes1"), (2, 3, None), (3, 4, None)):
-            grouped = sb("dw%d_grouped" % first, [P, 2 * P * (last - first)], F32, after=after)
-            turn("dw%d" % first, dw_sorted[first:last], grouped[:])
-            cols = slice(first * P, last * P)
+        for lo, hi, after in ((0, 2, "g_codes1"), (2, 3, None), (3, 4, None)):
+            grouped = sb("dw%d_grouped" % lo, [P, 2 * P * (hi - lo)], F32, after=after)
+            turn("dw%d" % lo, dw_sorted[lo:hi], grouped[:])
+            cols = slice(lo * P, hi * P)
             quantize(dw_codes[:, cols], dw_scales[:, cols], grouped)
-        gather((1,), "dw2_grouped")
+        gather((second,), "dw2_grouped")
 
-        def second_product(j, first, last, tag):
-            bank = psum.tile([P, last - first], F32, name="q_bank%d_%d" % (j, first), tag=tag)
+        def second_product(j, lo, hi, tag):
+            bank = psum.tile([P, hi - lo], F32, name="q_bank%d_%d" % (j, lo), tag=tag)
             nc.tensor.matmul_mx(
                 out=bank[:],
                 lhsT=pj_words[:, 2 * P * j : 2 * P * (j + 1)].bitcast(E2M1),
                 lhsT_scale=pj_scales[0][:] if j == 0 else pj_scales[1][:, P * (j - 1) : P * j],
-                rhs=dw_codes[:, first:last].bitcast(E4M3),
-                rhs_scale=dw_scales[:, first:last],
+                rhs=dw_codes[:, lo:hi].bitcast(E4M3),
+                rhs_scale=dw_scales[:, lo:hi],
                 start=True,
                 stop=True,
             )
-            nc.scalar.copy(out=q_sb[j][:, first:last], in_=bank[:])
+            nc.scalar.copy(out=q_sb[j][:, lo:hi], in_=bank[:])
 
         q_sb = [sb("q_sb%d" % j, [P, SLOTS], F32) for j in range(LANES)]
 
-        decay((0,), "dw_sorted2")
-        second_product(0, 0, HALF, "bank4")
-        second_product(0, HALF, 3 * P, "bank0")
-        second_product(0, 3 * P, SLOTS, "bank1")
-        second_product(1, 0, SLOTS, "bank2")
-        decay((1,), "pj_scales0")
-        second_product(2, 0, SLOTS, "bank3")
-        second_product(3, 0, SLOTS, "bank4")
-        decay((2, 3), "pj_scales1")
+        decay((first,), "dw_sorted3")
+        second_product(first, 0, HALF, "bank4")
+        second_product(first, HALF, 3 * P, "bank0")
+        second_product(first, 3 * P, SLOTS, "bank1")
+        second_product(second, 0, SLOTS, "bank2")
+        decay((second,), "pj_scales0")
+        second_product(third, 0, SLOTS, "bank3")
+        second_product(last, 0, SLOTS, "bank4")
+        late_out, late_in = decay((third, last), "pj_scales1", held_back=LATE)
 
-        def scatter(j):
-            nc.vector.tensor_tensor(m_new[j][:].indirect(offsets[:]), decayed[j], q_sb[j][:], ADD)
-
-        WIDE = COLS // 2
         QUARTER = COLS // 4
-        SPLIT = 416
         y_grouped = sb("y_grouped", [P, COLS * LANES], BF16)
         y_lanes = y_grouped[:].rearrange("p (n t) -> p n t", t=LANES)
         y_codes = [sb("y_codes%d" % s, [P, QUARTER], U32) for s in range(4)]
         y_scales = sb("y_scales", [P, COLS], U8)
 
-        def round_lane(copy, j, first, last):
-            copy(out=y_lanes[:, first:last, j], in_=m_new[j][:, first:last])
+        def round_lane(copy, j, lo, hi):
+            copy(out=y_lanes[:, lo:hi, j], in_=m_new[j][:, lo:hi])
 
-        for j in range(LANES):
-            scatter(j)
+        for j in ORDER:
+            nc.vector.tensor_tensor(m_new[j][:].indirect(offsets[:]), decayed[j], q_sb[j][:], ADD)
             nc.sync.dma_start(out=out_rows[:, j, :], in_=m_new[j][:])
-            if j < 3:
-                round_lane(nc.scalar.copy, j, 0 if j < 2 else SPLIT, COLS)
-        for first, last in ((SPLIT, WIDE), (WIDE, 3 * QUARTER), (3 * QUARTER, COLS)):
-            round_lane(nc.scalar.copy, 3, first, last)
-        round_lane(nc.vector.tensor_copy, 2, 0, SPLIT)
-        round_lane(nc.vector.tensor_copy, 3, 0, QUARTER)
-        round_lane(nc.vector.tensor_copy, 3, QUARTER, SPLIT)
+            if j != last:
+                round_lane(nc.scalar.copy, j, 0, COLS)
+            if j == first:
+                nc.scalar.mul(late_out, late_in, DECAY)
+        for lo, hi in ((SPLIT, 3 * QUARTER), (3 * QUARTER, COLS)):
+            round_lane(nc.scalar.copy, last, lo, hi)
+        for lo, hi in ((0, QUARTER), (QUARTER, 2 * QUARTER), (2 * QUARTER, SPLIT)):
+            round_lane(nc.vector.tensor_copy, last, lo, hi)
 
         words_out = out_1[0].rearrange("p n t -> p (n t)").bitcast(I32)
 

@@ -67,12 +67,13 @@ def tile_attend_glowmom_pl_kernel(
                 in_=Pj_scales[0, 4 * q : 4 * q + 4, :].bitcast(I32),
             )
         nc.sync.dma_start(out=x_raw[1][:], in_=x_rows[:, 2:4, :])
-        nc.sync.dma_start(out=pj_raw[:].bitcast(I32), in_=Pj_words[0].bitcast(I32))
         for u in range(2):
             nc.sync.dma_start(out=g_raw[u][:], in_=g_rows[:, 2 * u : 2 * u + 2, :])
         nc.sync.dma_start(offsets[:], offs)
-        for j in (first, third, last, second):
+        for j in (first, third, last):
             nc.sync.dma_start(out=m_src[j][:], in_=m_rows[:, j, :])
+        nc.sync.dma_start(out=pj_raw[:].bitcast(I32), in_=Pj_words[0].bitcast(I32))
+        nc.sync.dma_start(out=m_src[second][:], in_=m_rows[:, second, :])
         for j in ORDER:
             nc.sync.dma_start(out=m_new[j][:], in_=m_rows[:, j, :])
 
@@ -131,17 +132,12 @@ def tile_attend_glowmom_pl_kernel(
             return t[:, cut:], src[:, cut:]
 
         turn_x(0)
-        pj_words = sb("pj_words", [P, 2 * K], U8)
         pj_scales = [sb("pj_scales0", [P, P], U8), sb("pj_scales1", [P, K - P], U8)]
         pjs_lanes = pjs_raw[:].rearrange("p (m j) -> p j m", j=LANES)
         nc.vector.tensor_copy(out=pj_scales[0][:], in_=pjs_lanes[:, 0, :])
         nc.vector.tensor_copy(out=pj_scales[1][:].rearrange("p (j m) -> p j m", m=P), in_=pjs_lanes[:, 1:, :])
         turn_x(1)
         quantize_x(0)
-        nc.vector.tensor_copy(
-            out=pj_words[:].bitcast(U16).rearrange("p (j m) -> p j m", j=LANES),
-            in_=pj_raw[:].bitcast(U16).rearrange("p (m j) -> p j m", j=LANES),
-        )
 
         g_codes = [sb("g_codes%d" % h, [P, HALF], U32) for h in range(2)]
         g_scales = [sb("g_scales%d" % h, [P, HALF], U8) for h in range(2)]
@@ -204,18 +200,30 @@ def tile_attend_glowmom_pl_kernel(
             round_dw(n)
         dw_codes = sb("dw_codes", [P, SLOTS], U32)
         dw_scales = sb("dw_scales", [P, SLOTS], U8)
-        for lo, hi, after in ((0, 2, "g_codes1"), (2, 3, None), (3, 4, None)):
+        for lo, hi, after in ((0, 2, "g_codes1"), (2, 3, None), (3, 4, 8192)):
             grouped = sb("dw%d_grouped" % lo, [P, 2 * P * (hi - lo)], F32, after=after)
             turn("dw%d" % lo, dw_sorted[lo:hi], grouped[:])
             cols = slice(lo * P, hi * P)
             quantize(dw_codes[:, cols], dw_scales[:, cols], grouped)
         gather((second,), "dw2_grouped")
 
+        pj_lanes = pj_raw[:].rearrange("p (m j b) -> p j m b", j=LANES, b=2)
+        pj_words = [None] * LANES
+
+        def deal_words(j, after):
+            pj_words[j] = sb("pj_words%d" % j, [P, 2 * P], U8, after=after)
+            nc.gpsimd.tensor_copy(out=pj_words[j][:].rearrange("p (m b) -> p m b", b=2), in_=pj_lanes[:, j])
+
+        deal_words(first, None)
+        deal_words(second, None)
+        deal_words(third, 8192)
+        deal_words(last, 8192 + 512)
+
         def second_product(j, lo, hi, tag):
             bank = psum.tile([P, hi - lo], F32, name="q_bank%d_%d" % (j, lo), tag=tag)
             nc.tensor.matmul_mx(
                 out=bank[:],
-                lhsT=pj_words[:, 2 * P * j : 2 * P * (j + 1)].bitcast(E2M1),
+                lhsT=pj_words[j][:].bitcast(E2M1),
                 lhsT_scale=pj_scales[0][:] if j == 0 else pj_scales[1][:, P * (j - 1) : P * j],
                 rhs=dw_codes[:, lo:hi].bitcast(E4M3),
                 rhs_scale=dw_scales[:, lo:hi],

@@ -14,17 +14,16 @@ E5M2 = mybir.dt.float8_e5m2_x4
 E2M1 = mybir.dt.float4_e2m1fn_x4
 MULT = mybir.AluOpType.mult
 ADD = mybir.AluOpType.add
+COPY = mybir.ActivationFunctionType.Copy
 
 P = 128
 LANES = 4
 D = R = K = SLOTS = 512
 COLS = 1024
 HALF = SLOTS // 2
+QUARTER = COLS // 4
 DECAY = 0.9
-ORDER = (0, 2, 3, 1)
-LATE = 64
 G_SPLIT = 320
-SPLIT = 576
 FLOPS = 2 * D * R * SLOTS + 2 * K * D * SLOTS
 
 
@@ -42,7 +41,6 @@ def tile_attend_glowmom_pl_kernel(
                 return shared.tile(shape, dtype, name=name, offset=after, align_bytes=64)
             return keep.tile(shape, dtype, name=name, tag=after or name, align_bytes=64)
 
-        first, second, third, last = ORDER
         offsets = keep.tile([P, SLOTS // 16], U16, name="offsets")
         ident = sb("ident", [P, P], F32)
         x_raw = [sb("x_raw%d" % h, [P, 2, R], F32) for h in range(2)]
@@ -55,7 +53,7 @@ def tile_attend_glowmom_pl_kernel(
         m_rows = mT.rearrange("(p j) t -> p j t", j=LANES)
         out_rows = out_0.rearrange("(p j) t -> p j t", j=LANES)
         g_rows = G.rearrange("(p j) i -> p j i", j=LANES)
-        x_rows = xT.rearrange("(p c) r -> p c r", c=LANES)
+        x_rows = xT.rearrange("(p t) r -> p t r", t=LANES)
 
         nc.gpsimd.memset(pjs_raw[:].bitcast(I32), 0)
         make_identity(nc, ident[:])
@@ -70,78 +68,54 @@ def tile_attend_glowmom_pl_kernel(
         for u in range(2):
             nc.sync.dma_start(out=g_raw[u][:], in_=g_rows[:, 2 * u : 2 * u + 2, :])
         nc.sync.dma_start(offsets[:], offs)
-        for j in (first, third, last):
-            nc.sync.dma_start(out=m_src[j][:], in_=m_rows[:, j, :])
         nc.sync.dma_start(out=pj_raw[:].bitcast(I32), in_=Pj_words[0].bitcast(I32))
-        nc.sync.dma_start(out=m_src[second][:], in_=m_rows[:, second, :])
-        for j in ORDER:
-            nc.sync.dma_start(out=m_new[j][:], in_=m_rows[:, j, :])
+        for tiles, j in (
+            (m_src, 0), (m_src, 1), (m_src, 2), (m_new, 0), (m_src, 3), (m_new, 1), (m_new, 2), (m_new, 3)
+        ):
+            nc.sync.dma_start(out=tiles[j][:], in_=m_rows[:, j, :])
 
-        def turn(name, sorted_tiles, words_out):
-            n = len(sorted_tiles)
-            bank = psum.tile([P, n, 2, P], F32, name=name + "_bank", tag="turn", bufs=3)
-            for c in range(n):
-                words = sorted_tiles[c].bitcast(F32)
-                for u in range(2):
-                    nc.tensor.transpose(bank[:, c, u, :], words[:, u * P : (u + 1) * P], ident[:])
-            nc.scalar.copy(
-                out=words_out.rearrange("p (c n u) -> p c n u", c=n, u=2),
-                in_=bank[:].rearrange("p c u n -> p c n u"),
-            )
+        def half(h):
+            return slice(h * HALF, (h + 1) * HALF)
 
-        def quantize(codes, scales, grouped):
-            nc.vector.quantize_mx(out=codes.bitcast(E4M3), scales=scales, in_=grouped[:].bitcast(BF16))
-
-        def sort_pairs(copy, dst, src):
-            copy(
-                out=dst.rearrange("a (u p e) -> a u p e", u=2, e=2),
-                in_=src.rearrange("a (p u e) -> a u p e", u=2, e=2),
-            )
+        def block(b):
+            return slice(b * P, (b + 1) * P)
 
         x_codes = sb("x_codes", [P, D], U32)
         x_scales = sb("x_scales", [P, D], U8)
-
         x_grouped = [sb("x0_grouped", [P, 4 * P], F32, after=3072), sb("x1_grouped", [P, 4 * P], F32)]
 
         def turn_x(h):
             for c in range(2):
-                t = sb("x_sorted%d%d" % (h, c), [P, R], BF16)
-                sort_pairs(nc.vector.tensor_copy, t[:], x_raw[h][:, c, :])
-                turn("x%d%d" % (h, c), [t[:]], x_grouped[h][:, 2 * P * c : 2 * P * (c + 1)])
+                rounded = sb("x_sorted%d%d" % (h, c), [P, R], BF16)
+                nc.vector.tensor_copy(
+                    out=rounded[:].rearrange("a (u p e) -> a u p e", u=2, e=2),
+                    in_=x_raw[h][:, c, :].rearrange("a (p u e) -> a u p e", u=2, e=2),
+                )
+                bank = psum.tile([P, 2, P], F32, name="x_bank%d%d" % (h, c), tag="bank%d" % (4 + 2 * h + c))
+                words = rounded[:].bitcast(F32)
+                for u in range(2):
+                    nc.tensor.transpose(bank[:, u, :], words[:, block(u)], ident[:])
+                nc.scalar.copy(
+                    out=x_grouped[h][:, half(c)].rearrange("p (n u) -> p n u", u=2),
+                    in_=bank[:].rearrange("p u n -> p n u"),
+                )
 
         def quantize_x(h):
-            cols = slice(h * 2 * P, (h + 1) * 2 * P)
-            quantize(x_codes[:, cols], x_scales[:, cols], x_grouped[h])
-
-        picked = [None] * LANES
-        decayed = [None] * LANES
-
-        def gather(lanes, after):
-            t = sb("picked%d" % lanes[0], [P, len(lanes), SLOTS], F32, after=after)
-            for n, j in enumerate(lanes):
-                nc.vector.tensor_copy(t[:, n, :], m_src[j][:].indirect(offsets[:]))
-            picked[lanes[0]] = t
-
-        def decay(lanes, after, held_back=0):
-            t = sb("decayed%d" % lanes[0], [P, len(lanes) * SLOTS], F32, after=after)
-            src = picked[lanes[0]][:].rearrange("p n i -> p (n i)")
-            cut = len(lanes) * SLOTS - held_back
-            nc.scalar.mul(t[:, :cut], src[:, :cut], DECAY)
-            for n, j in enumerate(lanes):
-                decayed[j] = t[:, n * SLOTS : (n + 1) * SLOTS]
-            return t[:, cut:], src[:, cut:]
+            nc.vector.quantize_mx(
+                out=x_codes[:, half(h)].bitcast(E4M3), scales=x_scales[:, half(h)], in_=x_grouped[h][:].bitcast(BF16)
+            )
 
         turn_x(0)
-        pj_scales = [sb("pj_scales0", [P, P], U8), sb("pj_scales1", [P, K - P], U8)]
-        pjs_lanes = pjs_raw[:].rearrange("p (m j) -> p j m", j=LANES)
-        nc.vector.tensor_copy(out=pj_scales[0][:], in_=pjs_lanes[:, 0, :])
-        nc.vector.tensor_copy(out=pj_scales[1][:].rearrange("p (j m) -> p j m", m=P), in_=pjs_lanes[:, 1:, :])
+        pj_scales = sb("pj_scales", [P, K], U8)
+        nc.vector.tensor_copy(
+            out=pj_scales[:].rearrange("p (j m) -> p j m", j=LANES),
+            in_=pjs_raw[:].rearrange("p (m j) -> p j m", j=LANES),
+        )
         turn_x(1)
         quantize_x(0)
 
         g_codes = [sb("g_codes%d" % h, [P, HALF], U32) for h in range(2)]
         g_scales = [sb("g_scales%d" % h, [P, HALF], U8) for h in range(2)]
-
         g_grouped = [sb("g_grouped%d" % h, [P, HALF * LANES], BF16, after=2048 * (h + 1)) for h in range(2)]
 
         def group_g(copy, u, lo, hi):
@@ -167,119 +141,144 @@ def tile_attend_glowmom_pl_kernel(
         quantize_g(0, P)
         quantize_g(P, HALF)
         quantize_g(HALF, SLOTS)
-        gather((first,), 1024)
-        gather((third, last), 4096)
+        pj_words = sb("pj_words", [P, 2 * K], U8, after="x1_grouped")
+        nc.scalar.copy(
+            out=pj_words[:].bitcast(U16).rearrange("p (j m) -> p j m", j=LANES),
+            in_=pj_raw[:].bitcast(U16).rearrange("p (m j) -> p j m", j=LANES),
+        )
 
-        dw_sorted = []
+        dw_codes = [sb("dw_codes%d" % h, [P, HALF], U32) for h in range(2)]
+        dw_scales = [sb("dw_scales%d" % h, [P, HALF], U8) for h in range(2)]
+        dw_grouped = [sb("dw_grouped0", [P, HALF * LANES], BF16, after=8192), sb("dw_grouped1", [P, HALF * LANES], BF16)]
 
-        def first_product(n):
-            h, cols = n // 2, slice(n % 2 * P, (n % 2 + 1) * P)
-            bank = psum.tile([P, D], F32, name="dw_bank%d" % n, tag="bank%d" % n)
-            nc.tensor.matmul_mx(
-                out=bank[:],
-                lhsT=g_codes[h][:, cols].bitcast(E5M2),
-                lhsT_scale=g_scales[h][:, cols],
-                rhs=x_codes[:].bitcast(E4M3),
-                rhs_scale=x_scales[:],
-                start=True,
-                stop=True,
-            )
-            return bank
-
-        def round_dw(n):
-            bank = dw_banks[n]
-            t = sb("dw_sorted%d" % n, [P, D], BF16)
+        def first_product(b):
+            bank = psum.tile([P, LANES, P], F32, name="dw_bank%d" % b, tag="bank%d" % b)
+            for t in range(LANES):
+                nc.tensor.matmul_mx(
+                    out=bank[:, t, :],
+                    lhsT=x_codes[:, block(t)].bitcast(E4M3),
+                    lhsT_scale=x_scales[:, block(t)],
+                    rhs=g_codes[b // 2][:, block(b % 2)].bitcast(E5M2),
+                    rhs_scale=g_scales[b // 2][:, block(b % 2)],
+                    start=True,
+                    stop=True,
+                )
             nc.scalar.copy(
-                out=t[:].rearrange("a (u p e) -> a u p e", u=2, e=2),
-                in_=bank[:].rearrange("a (u e p) -> a u p e", u=2, e=2),
+                out=dw_grouped[b // 2][:, b % 2 * SLOTS : (b % 2 + 1) * SLOTS].rearrange("p (n t) -> p n t", t=LANES),
+                in_=bank[:].rearrange("p t n -> p n t"),
             )
-            dw_sorted.append(t[:])
 
-        dw_banks = [first_product(n) for n in range(4)]
-        for n in range(4):
-            round_dw(n)
-        dw_codes = sb("dw_codes", [P, SLOTS], U32)
-        dw_scales = sb("dw_scales", [P, SLOTS], U8)
-        for lo, hi, after in ((0, 2, "g_codes1"), (2, 3, None), (3, 4, 8192)):
-            grouped = sb("dw%d_grouped" % lo, [P, 2 * P * (hi - lo)], F32, after=after)
-            turn("dw%d" % lo, dw_sorted[lo:hi], grouped[:])
-            cols = slice(lo * P, hi * P)
-            quantize(dw_codes[:, cols], dw_scales[:, cols], grouped)
-        gather((second,), "dw2_grouped")
+        q_banks = {}
 
-        pj_lanes = pj_raw[:].rearrange("p (m j b) -> p j m b", j=LANES, b=2)
-        pj_words = [None] * LANES
+        def second_product(h, lanes):
+            nc.vector.quantize_mx(out=dw_codes[h][:].bitcast(E4M3), scales=dw_scales[h][:], in_=dw_grouped[h][:])
+            for j in lanes:
+                bank = psum.tile([P, HALF], F32, name="q_bank%d_%d" % (j, h), tag="bank%d" % (4 - 4 * h + j))
+                nc.tensor.matmul_mx(
+                    out=bank[:],
+                    lhsT=pj_words[:, 2 * P * j : 2 * P * (j + 1)].bitcast(E2M1),
+                    lhsT_scale=pj_scales[:, block(j)],
+                    rhs=dw_codes[h][:].bitcast(E4M3),
+                    rhs_scale=dw_scales[h][:],
+                    start=True,
+                    stop=True,
+                )
+                q_banks[j, h] = bank
 
-        def deal_words(j, after):
-            pj_words[j] = sb("pj_words%d" % j, [P, 2 * P], U8, after=after)
-            nc.gpsimd.tensor_copy(out=pj_words[j][:].rearrange("p (m b) -> p m b", b=2), in_=pj_lanes[:, j])
+        picked = {}
+        updated = {}
 
-        deal_words(first, None)
-        deal_words(second, None)
-        deal_words(third, 8192)
-        deal_words(last, 8192 + 512)
+        def listed(lo, hi):
+            return offsets[:, lo // 16 : hi // 16]
 
-        def second_product(j, lo, hi, tag):
-            bank = psum.tile([P, hi - lo], F32, name="q_bank%d_%d" % (j, lo), tag=tag)
-            nc.tensor.matmul_mx(
-                out=bank[:],
-                lhsT=pj_words[j][:].bitcast(E2M1),
-                lhsT_scale=pj_scales[0][:] if j == 0 else pj_scales[1][:, P * (j - 1) : P * j],
-                rhs=dw_codes[:, lo:hi].bitcast(E4M3),
-                rhs_scale=dw_scales[:, lo:hi],
-                start=True,
-                stop=True,
-            )
-            nc.scalar.copy(out=q_sb[j][:, lo:hi], in_=bank[:])
+        def scalar_move(out, in_):
+            nc.scalar.activation(out, in_, COPY)
 
-        q_sb = [sb("q_sb%d" % j, [P, SLOTS], F32) for j in range(LANES)]
+        def gather(copy, j, h, after=None):
+            picked[j, h] = sb("picked%d_%d" % (j, h), [P, HALF], F32, after=after)
+            copy(picked[j, h][:], m_src[j][:].indirect(listed(h * HALF, (h + 1) * HALF)))
 
-        decay((first,), "dw_sorted3")
-        second_product(first, 0, HALF, "bank4")
-        second_product(first, HALF, 3 * P, "bank0")
-        second_product(first, 3 * P, SLOTS, "bank1")
-        second_product(second, 0, SLOTS, "bank2")
-        decay((second,), "pj_scales0")
-        second_product(third, 0, SLOTS, "bank3")
-        second_product(last, 0, SLOTS, "bank4")
-        late_out, late_in = decay((third, last), "pj_scales1", held_back=LATE)
+        def update(j, h, into=None):
+            updated[j, h] = sb("updated%d_%d" % (j, h), [P, HALF], F32)[:] if into is None else into
+            nc.vector.scalar_tensor_tensor(updated[j, h], picked[j, h][:], DECAY, q_banks[j, h][:], MULT, ADD)
 
-        QUARTER = COLS // 4
-        y_grouped = sb("y_grouped", [P, COLS * LANES], BF16)
-        y_lanes = y_grouped[:].rearrange("p (n t) -> p n t", t=LANES)
+        def scatter(copy, j, h):
+            copy(m_new[j][:].indirect(listed(h * HALF, (h + 1) * HALF)), updated[j, h])
+
+        y_words = sb("y_words", [P, 2, COLS * 2], BF16)
+
+        def pair_lane(j):
+            return y_words[:, j // 2, :].rearrange("p (n e) -> p n e", e=2)[:, :, j % 2]
+
+        def store_lane(j):
+            nc.sync.dma_start(out=out_rows[:, j, :], in_=m_new[j][:])
+
+        def finish_early(j):
+            store_lane(j)
+            nc.gpsimd.tensor_scalar(pair_lane(j), m_new[j][:], 1.0, 0.0, MULT, ADD)
+
+        for b in range(4):
+            first_product(b)
+        gather(nc.vector.tensor_copy, 0, 0, after=2048)
+        gather(nc.vector.tensor_copy, 0, 1, after=4096)
+        gather(nc.vector.tensor_copy, 1, 0, after=5120)
+        second_product(0, range(LANES))
+        gather(nc.vector.tensor_copy, 1, 1, after=8192)
+        gather(scalar_move, 2, 0, after=8192 + 1024)
+        update(0, 0)
+        scatter(scalar_move, 0, 0)
+        second_product(1, range(LANES))
+        whole = sb("updated1", [P, SLOTS], F32)
+        update(1, 0, whole[:, half(0)])
+        gather(scalar_move, 2, 1, after=5120)
+        update(2, 0)
+        update(0, 1)
+        scatter(scalar_move, 0, 1)
+        finish_early(0)
+        update(1, 1, whole[:, half(1)])
+        gather(nc.vector.tensor_copy, 3, 0)
+        gather(nc.vector.tensor_copy, 3, 1)
+        update(2, 1)
+        update(3, 0)
+        update(3, 1)
+        nc.vector.tensor_copy(m_new[1][:].indirect(offsets[:]), whole[:])
+        finish_early(1)
+        scatter(scalar_move, 2, 0)
+        scatter(nc.vector.tensor_copy, 2, 1)
+        store_lane(2)
+        scatter(scalar_move, 3, 0)
+        scatter(scalar_move, 3, 1)
+        store_lane(3)
+        nc.vector.tensor_copy(out=pair_lane(2), in_=m_new[2][:])
+        nc.vector.tensor_copy(out=pair_lane(3), in_=m_new[3][:])
+
+        y_grouped = [sb("y_grouped%d" % s, [P, QUARTER * 2], F32) for s in range(4)]
         y_codes = [sb("y_codes%d" % s, [P, QUARTER], U32) for s in range(4)]
         y_scales = sb("y_scales", [P, COLS], U8)
-
-        def round_lane(copy, j, lo, hi):
-            copy(out=y_lanes[:, lo:hi, j], in_=m_new[j][:, lo:hi])
-
-        for j in ORDER:
-            nc.vector.tensor_tensor(m_new[j][:].indirect(offsets[:]), decayed[j], q_sb[j][:], ADD)
-            nc.sync.dma_start(out=out_rows[:, j, :], in_=m_new[j][:])
-            if j != last:
-                round_lane(nc.scalar.copy, j, 0, COLS)
-            if j == first:
-                nc.scalar.mul(late_out, late_in, DECAY)
-        for lo, hi in ((SPLIT, 3 * QUARTER), (3 * QUARTER, COLS)):
-            round_lane(nc.scalar.copy, last, lo, hi)
-        for lo, hi in ((0, QUARTER), (QUARTER, 2 * QUARTER), (2 * QUARTER, SPLIT)):
-            round_lane(nc.vector.tensor_copy, last, lo, hi)
-
         words_out = out_1[0].rearrange("p n t -> p (n t)").bitcast(I32)
 
-        def store_scales(queue, q):
-            queue.dma_start(
+        def weave(copy, s):
+            cols = slice(s * QUARTER, (s + 1) * QUARTER)
+            copy(
+                out=y_grouped[s][:].rearrange("p (n u) -> p n u", u=2),
+                in_=y_words[:].bitcast(F32)[:, :, cols].rearrange("p u n -> p n u"),
+            )
+
+        def quantize_y(s):
+            cols = slice(s * QUARTER, (s + 1) * QUARTER)
+            nc.vector.quantize_mx(
+                out=y_codes[s][:].bitcast(E4M3), scales=y_scales[:, cols], in_=y_grouped[s][:].bitcast(BF16)
+            )
+            nc.sync.dma_start(out=words_out[:, cols], in_=y_codes[s][:].bitcast(I32))
+
+        weave(nc.scalar.copy, 2)
+        weave(nc.scalar.copy, 3)
+        weave(nc.vector.tensor_copy, 0)
+        weave(nc.vector.tensor_copy, 1)
+        for s in range(4):
+            quantize_y(s)
+        for q in range(4):
+            (nc.scalar, nc.sync)[q % 2].dma_start(
                 out=out_2[0, 4 * q : 4 * q + 4, :].bitcast(I32),
                 in_=y_scales[32 * q : 32 * q + 4, :].bitcast(I32),
             )
-
-        for s in range(4):
-            cols = slice(s * QUARTER, (s + 1) * QUARTER)
-            nc.vector.quantize_mx(
-                out=y_codes[s][:].bitcast(E4M3),
-                scales=y_scales[:, cols],
-                in_=y_grouped[:, s * QUARTER * LANES : (s + 1) * QUARTER * LANES],
-            )
-            nc.sync.dma_start(out=words_out[:, cols], in_=y_codes[s][:].bitcast(I32))
-        for q in range(4):
-            store_scales((nc.scalar, nc.sync)[q % 2], q)

@@ -23,7 +23,8 @@ COLS = 1024
 HALF = SLOTS // 2
 QUARTER = COLS // 4
 DECAY = 0.9
-G_SPLIT = 320
+G_SPLIT = 288
+SHARE = 288
 FLOPS = 2 * D * R * SLOTS + 2 * K * D * SLOTS
 
 
@@ -68,9 +69,10 @@ def tile_attend_glowmom_pl_kernel(
         for u in range(2):
             nc.sync.dma_start(out=g_raw[u][:], in_=g_rows[:, 2 * u : 2 * u + 2, :])
         nc.sync.dma_start(offsets[:], offs)
+        nc.sync.dma_start(out=m_src[0][:], in_=m_rows[:, 0, :])
         nc.sync.dma_start(out=pj_raw[:].bitcast(I32), in_=Pj_words[0].bitcast(I32))
         for tiles, j in (
-            (m_src, 0), (m_src, 1), (m_src, 2), (m_new, 0), (m_src, 3), (m_new, 1), (m_new, 2), (m_new, 3)
+            (m_src, 1), (m_src, 3), (m_new, 0), (m_new, 1), (m_src, 2), (m_new, 2), (m_new, 3)
         ):
             nc.sync.dma_start(out=tiles[j][:], in_=m_rows[:, j, :])
 
@@ -114,38 +116,25 @@ def tile_attend_glowmom_pl_kernel(
         turn_x(1)
         quantize_x(0)
 
-        g_codes = [sb("g_codes%d" % h, [P, HALF], U32) for h in range(2)]
-        g_scales = [sb("g_scales%d" % h, [P, HALF], U8) for h in range(2)]
-        g_grouped = [sb("g_grouped%d" % h, [P, HALF * LANES], BF16, after=2048 * (h + 1)) for h in range(2)]
+        g_pieces = ((0, P), (P, HALF), (HALF, SLOTS))
+        g_codes = [sb("g_codes%d" % lo, [P, hi - lo], U32) for lo, hi in g_pieces]
+        g_scales = [sb("g_scales%d" % lo, [P, hi - lo], U8) for lo, hi in g_pieces]
+        g_grouped = [sb("g_grouped%d" % lo, [P, (hi - lo) * LANES], BF16, after=2560 + 8 * lo) for lo, hi in g_pieces]
 
-        def group_g(copy, u, lo, hi):
-            h, cols = lo // HALF, slice(lo % HALF, lo % HALF + hi - lo)
-            pairs = g_grouped[h][:].rearrange("p (i u e) -> p u i e", u=2, e=2)
-            copy(out=pairs[:, u, cols, :], in_=g_raw[u][:, :, lo:hi].rearrange("p e i -> p i e"))
+        def group_g(copy, u, n, lo, hi):
+            first = g_pieces[n][0]
+            pairs = g_grouped[n][:].rearrange("p (i u e) -> p u i e", u=2, e=2)
+            copy(out=pairs[:, u, lo - first : hi - first], in_=g_raw[u][:, :, lo:hi].rearrange("p e i -> p i e"))
 
-        def quantize_g(lo, hi):
-            h, cols = lo // HALF, slice(lo % HALF, lo % HALF + hi - lo)
-            nc.vector.quantize_mx(
-                out=g_codes[h][:, cols].bitcast(E5M2),
-                scales=g_scales[h][:, cols],
-                in_=g_grouped[h][:, LANES * cols.start : LANES * cols.stop],
-            )
-
-        group_g(nc.vector.tensor_copy, 0, 0, HALF)
-        group_g(nc.vector.tensor_copy, 0, HALF, SLOTS)
+        for n, (lo, hi) in enumerate(g_pieces):
+            group_g(nc.vector.tensor_copy, 0, n, lo, hi)
         quantize_x(1)
-        group_g(nc.scalar.copy, 1, G_SPLIT, SLOTS)
-        group_g(nc.vector.tensor_copy, 1, 0, P)
-        group_g(nc.vector.tensor_copy, 1, P, HALF)
-        group_g(nc.vector.tensor_copy, 1, HALF, G_SPLIT)
-        quantize_g(0, P)
-        quantize_g(P, HALF)
-        quantize_g(HALF, SLOTS)
-        pj_words = sb("pj_words", [P, 2 * K], U8, after="x1_grouped")
-        nc.scalar.copy(
-            out=pj_words[:].bitcast(U16).rearrange("p (j m) -> p j m", j=LANES),
-            in_=pj_raw[:].bitcast(U16).rearrange("p (m j) -> p j m", j=LANES),
-        )
+        group_g(nc.scalar.copy, 1, 2, G_SPLIT, SLOTS)
+        group_g(nc.vector.tensor_copy, 1, 0, 0, P)
+        group_g(nc.vector.tensor_copy, 1, 1, P, HALF)
+        group_g(nc.vector.tensor_copy, 1, 2, HALF, G_SPLIT)
+        for n in range(3):
+            nc.vector.quantize_mx(out=g_codes[n][:].bitcast(E5M2), scales=g_scales[n][:], in_=g_grouped[n][:])
 
         dw_codes = [sb("dw_codes%d" % h, [P, HALF], U32) for h in range(2)]
         dw_scales = [sb("dw_scales%d" % h, [P, HALF], U8) for h in range(2)]
@@ -153,13 +142,14 @@ def tile_attend_glowmom_pl_kernel(
 
         def first_product(b):
             bank = psum.tile([P, LANES, P], F32, name="dw_bank%d" % b, tag="bank%d" % b)
+            n, cols = min(b, 2), block(max(b - 2, 0))
             for t in range(LANES):
                 nc.tensor.matmul_mx(
                     out=bank[:, t, :],
                     lhsT=x_codes[:, block(t)].bitcast(E4M3),
                     lhsT_scale=x_scales[:, block(t)],
-                    rhs=g_codes[b // 2][:, block(b % 2)].bitcast(E5M2),
-                    rhs_scale=g_scales[b // 2][:, block(b % 2)],
+                    rhs=g_codes[n][:, cols].bitcast(E5M2),
+                    rhs_scale=g_scales[n][:, cols],
                     start=True,
                     stop=True,
                 )
@@ -170,12 +160,15 @@ def tile_attend_glowmom_pl_kernel(
 
         q_banks = {}
 
-        def second_product(h, lanes):
+        def quantize_dw(h):
             nc.vector.quantize_mx(out=dw_codes[h][:].bitcast(E4M3), scales=dw_scales[h][:], in_=dw_grouped[h][:])
+
+        def second_product(h, lanes):
             for j in lanes:
                 bank = psum.tile([P, HALF], F32, name="q_bank%d_%d" % (j, h), tag="bank%d" % (4 - 4 * h + j))
+                q_banks[j, h] = bank[:]
                 nc.tensor.matmul_mx(
-                    out=bank[:],
+                    out=q_banks[j, h],
                     lhsT=pj_words[:, 2 * P * j : 2 * P * (j + 1)].bitcast(E2M1),
                     lhsT_scale=pj_scales[:, block(j)],
                     rhs=dw_codes[h][:].bitcast(E4M3),
@@ -183,7 +176,6 @@ def tile_attend_glowmom_pl_kernel(
                     start=True,
                     stop=True,
                 )
-                q_banks[j, h] = bank
 
         picked = {}
         updated = {}
@@ -195,12 +187,12 @@ def tile_attend_glowmom_pl_kernel(
             nc.scalar.activation(out, in_, COPY)
 
         def gather(copy, j, h, after=None):
-            picked[j, h] = sb("picked%d_%d" % (j, h), [P, HALF], F32, after=after)
-            copy(picked[j, h][:], m_src[j][:].indirect(listed(h * HALF, (h + 1) * HALF)))
+            picked[j, h] = sb("picked%d_%d" % (j, h), [P, HALF], F32, after=after)[:]
+            copy(picked[j, h], m_src[j][:].indirect(listed(h * HALF, (h + 1) * HALF)))
 
         def update(j, h, into=None):
             updated[j, h] = sb("updated%d_%d" % (j, h), [P, HALF], F32)[:] if into is None else into
-            nc.vector.scalar_tensor_tensor(updated[j, h], picked[j, h][:], DECAY, q_banks[j, h][:], MULT, ADD)
+            nc.vector.scalar_tensor_tensor(updated[j, h], picked[j, h], DECAY, q_banks[j, h], MULT, ADD)
 
         def scatter(copy, j, h):
             copy(m_new[j][:].indirect(listed(h * HALF, (h + 1) * HALF)), updated[j, h])
@@ -217,40 +209,49 @@ def tile_attend_glowmom_pl_kernel(
             store_lane(j)
             nc.gpsimd.tensor_scalar(pair_lane(j), m_new[j][:], 1.0, 0.0, MULT, ADD)
 
+        gather(scalar_move, 0, 0, after=2560)
         for b in range(4):
             first_product(b)
-        gather(nc.vector.tensor_copy, 0, 0, after=2048)
-        gather(nc.vector.tensor_copy, 0, 1, after=4096)
-        gather(nc.vector.tensor_copy, 1, 0, after=5120)
-        second_product(0, range(LANES))
-        gather(nc.vector.tensor_copy, 1, 1, after=8192)
-        gather(scalar_move, 2, 0, after=8192 + 1024)
+        gather(nc.vector.tensor_copy, 0, 1, after=3584)
+        pj_words = sb("pj_words", [P, 2 * K], U8, after=4608)
+        nc.vector.tensor_copy(
+            out=pj_words[:].bitcast(U16).rearrange("p (j m) -> p j m", j=LANES),
+            in_=pj_raw[:].bitcast(U16).rearrange("p (m j) -> p j m", j=LANES),
+        )
+        gather(nc.vector.tensor_copy, 1, 0, after=5632)
+        quantize_dw(0)
+        second_product(0, (0, 1, 3, 2))
+        gather(nc.vector.tensor_copy, 1, 1, after=8192 + 64)
+        gather(scalar_move, 3, 0, after=8192 + 1024 + 64)
+        quantize_dw(1)
         update(0, 0)
         scatter(scalar_move, 0, 0)
-        second_product(1, range(LANES))
-        whole = sb("updated1", [P, SLOTS], F32)
-        update(1, 0, whole[:, half(0)])
-        gather(scalar_move, 2, 1, after=5120)
-        update(2, 0)
+        second_product(1, (0, 1, 3, 2))
+        updated_1 = sb("updated1", [P, SLOTS], F32)
+        update(1, 0, updated_1[:, half(0)])
+        gather(scalar_move, 3, 1, after=5632)
         update(0, 1)
         scatter(scalar_move, 0, 1)
         finish_early(0)
-        update(1, 1, whole[:, half(1)])
-        gather(nc.vector.tensor_copy, 3, 0)
-        gather(nc.vector.tensor_copy, 3, 1)
-        update(2, 1)
-        update(3, 0)
-        update(3, 1)
-        nc.vector.tensor_copy(m_new[1][:].indirect(offsets[:]), whole[:])
+        update(1, 1, updated_1[:, half(1)])
+        update(3, 0, sb("updated3_0", [P, HALF], F32, after=3584)[:])
+        nc.vector.tensor_copy(m_new[1][:].indirect(listed(SHARE, SLOTS)), updated_1[:, SHARE:])
+        scalar_move(m_new[1][:].indirect(listed(0, SHARE)), updated_1[:, :SHARE])
         finish_early(1)
-        scatter(scalar_move, 2, 0)
-        scatter(nc.vector.tensor_copy, 2, 1)
+        gather(nc.vector.tensor_copy, 2, 0, after=8192 + 64)
+        gather(nc.vector.tensor_copy, 2, 1, after=8192 + 1024 + 64)
+        updated_2 = sb("updated2", [P, SLOTS], F32)
+        update(2, 0, updated_2[:, half(0)])
+        update(2, 1, updated_2[:, half(1)])
+        update(3, 1, sb("updated3_1", [P, HALF], F32, after=8192 + 64)[:])
+        nc.vector.tensor_copy(m_new[2][:].indirect(offsets[:]), updated_2[:])
         store_lane(2)
         scatter(scalar_move, 3, 0)
         scatter(scalar_move, 3, 1)
         store_lane(3)
         nc.vector.tensor_copy(out=pair_lane(2), in_=m_new[2][:])
-        nc.vector.tensor_copy(out=pair_lane(3), in_=m_new[3][:])
+        for lo, hi in ((0, QUARTER), (QUARTER, COLS)):
+            nc.vector.tensor_copy(out=pair_lane(3)[:, lo:hi], in_=m_new[3][:, lo:hi])
 
         y_grouped = [sb("y_grouped%d" % s, [P, QUARTER * 2], F32) for s in range(4)]
         y_codes = [sb("y_codes%d" % s, [P, QUARTER], U32) for s in range(4)]
@@ -271,11 +272,10 @@ def tile_attend_glowmom_pl_kernel(
             )
             nc.sync.dma_start(out=words_out[:, cols], in_=y_codes[s][:].bitcast(I32))
 
-        weave(nc.scalar.copy, 2)
-        weave(nc.scalar.copy, 3)
-        weave(nc.vector.tensor_copy, 0)
-        weave(nc.vector.tensor_copy, 1)
-        for s in range(4):
+        for s in range(3):
+            weave(nc.scalar.copy, s)
+        weave(nc.vector.tensor_copy, 3)
+        for s in (0, 3, 1, 2):
             quantize_y(s)
         for q in range(4):
             (nc.scalar, nc.sync)[q % 2].dma_start(

@@ -24,7 +24,7 @@ HALF = SLOTS // 2
 QUARTER = COLS // 4
 DECAY = 0.9
 G_SPLIT = 288
-SHARE = 288
+SHARE = 224
 FLOPS = 2 * D * R * SLOTS + 2 * K * D * SLOTS
 
 
@@ -138,7 +138,7 @@ def tile_attend_glowmom_pl_kernel(
 
         dw_codes = [sb("dw_codes%d" % h, [P, HALF], U32) for h in range(2)]
         dw_scales = [sb("dw_scales%d" % h, [P, HALF], U8) for h in range(2)]
-        dw_grouped = [sb("dw_grouped0", [P, HALF * LANES], BF16, after=8192), sb("dw_grouped1", [P, HALF * LANES], BF16)]
+        dw_grouped = [sb("dw_grouped0", [P, HALF * LANES], BF16, after=8192), sb("dw_grouped1", [P, HALF * LANES], BF16, after=12288)]
 
         def first_product(b):
             bank = psum.tile([P, LANES, P], F32, name="dw_bank%d" % b, tag="bank%d" % b)
@@ -209,41 +209,41 @@ def tile_attend_glowmom_pl_kernel(
             store_lane(j)
             nc.gpsimd.tensor_scalar(pair_lane(j), m_new[j][:], 1.0, 0.0, MULT, ADD)
 
-        gather(scalar_move, 0, 0, after=2560)
+        gather(scalar_move, 0, 0, after=2496)
         for b in range(4):
             first_product(b)
-        gather(nc.vector.tensor_copy, 0, 1, after=3584)
-        pj_words = sb("pj_words", [P, 2 * K], U8, after=4608)
+        gather(nc.vector.tensor_copy, 0, 1, after=3520)
+        pj_words = sb("pj_words", [P, 2 * K], U8, after=4544)
         nc.vector.tensor_copy(
             out=pj_words[:].bitcast(U16).rearrange("p (j m) -> p j m", j=LANES),
             in_=pj_raw[:].bitcast(U16).rearrange("p (m j) -> p j m", j=LANES),
         )
-        gather(nc.vector.tensor_copy, 1, 0, after=5632)
+        gather(nc.vector.tensor_copy, 1, 0, after=5568)
+        gather(nc.vector.tensor_copy, 1, 1, after=6592)
         quantize_dw(0)
         second_product(0, (0, 1, 3, 2))
-        gather(nc.vector.tensor_copy, 1, 1, after=8192 + 64)
         gather(scalar_move, 3, 0, after=8192 + 1024 + 64)
         quantize_dw(1)
-        update(0, 0)
+        update(0, 0, sb("updated0_0", [P, HALF], F32, after=12288)[:])
         scatter(scalar_move, 0, 0)
         second_product(1, (0, 1, 3, 2))
-        updated_1 = sb("updated1", [P, SLOTS], F32)
+        updated_1 = sb("updated1", [P, SLOTS], F32, after=13312)
         update(1, 0, updated_1[:, half(0)])
-        gather(scalar_move, 3, 1, after=5632)
+        gather(scalar_move, 3, 1, after=5568)
         update(0, 1)
         scatter(scalar_move, 0, 1)
         finish_early(0)
         update(1, 1, updated_1[:, half(1)])
-        update(3, 0, sb("updated3_0", [P, HALF], F32, after=3584)[:])
+        update(3, 0, sb("updated3_0", [P, HALF], F32, after=3520)[:])
         nc.vector.tensor_copy(m_new[1][:].indirect(listed(SHARE, SLOTS)), updated_1[:, SHARE:])
         scalar_move(m_new[1][:].indirect(listed(0, SHARE)), updated_1[:, :SHARE])
         finish_early(1)
-        gather(nc.vector.tensor_copy, 2, 0, after=8192 + 64)
+        gather(nc.vector.tensor_copy, 2, 0, after=6656)
         gather(nc.vector.tensor_copy, 2, 1, after=8192 + 1024 + 64)
         updated_2 = sb("updated2", [P, SLOTS], F32)
         update(2, 0, updated_2[:, half(0)])
         update(2, 1, updated_2[:, half(1)])
-        update(3, 1, sb("updated3_1", [P, HALF], F32, after=8192 + 64)[:])
+        update(3, 1, sb("updated3_1", [P, HALF], F32, after=6656)[:])
         nc.vector.tensor_copy(m_new[2][:].indirect(offsets[:]), updated_2[:])
         store_lane(2)
         scatter(scalar_move, 3, 0)

@@ -24,7 +24,8 @@ HALF = SLOTS // 2
 QUARTER = COLS // 4
 DECAY = 0.9
 G_SPLIT = 288
-SHARE = 224
+SHARE = 256
+LONG = 384
 FLOPS = 2 * D * R * SLOTS + 2 * K * D * SLOTS
 
 
@@ -60,12 +61,12 @@ def tile_attend_glowmom_pl_kernel(
         make_identity(nc, ident[:])
 
         nc.sync.dma_start(out=x_raw[0][:], in_=x_rows[:, 0:2, :])
+        nc.sync.dma_start(out=x_raw[1][:], in_=x_rows[:, 2:4, :])
         for q in range(4):
             nc.sync.dma_start(
                 out=pjs_raw[32 * q : 32 * q + 4, :].bitcast(I32),
                 in_=Pj_scales[0, 4 * q : 4 * q + 4, :].bitcast(I32),
             )
-        nc.sync.dma_start(out=x_raw[1][:], in_=x_rows[:, 2:4, :])
         for u in range(2):
             nc.sync.dma_start(out=g_raw[u][:], in_=g_rows[:, 2 * u : 2 * u + 2, :])
         nc.sync.dma_start(offsets[:], offs)
@@ -158,15 +159,17 @@ def tile_attend_glowmom_pl_kernel(
                 in_=bank[:].rearrange("p t n -> p n t"),
             )
 
-        q_banks = {}
+        q_last = psum.tile([P, SLOTS], F32, name="q_bank3", tag="bank7")
+        q_banks = {(3, h): q_last[:, half(h)] for h in range(2)}
 
         def quantize_dw(h):
             nc.vector.quantize_mx(out=dw_codes[h][:].bitcast(E4M3), scales=dw_scales[h][:], in_=dw_grouped[h][:])
 
         def second_product(h, lanes):
             for j in lanes:
-                bank = psum.tile([P, HALF], F32, name="q_bank%d_%d" % (j, h), tag="bank%d" % (4 - 4 * h + j))
-                q_banks[j, h] = bank[:]
+                if (j, h) not in q_banks:
+                    bank = psum.tile([P, HALF], F32, name="q_bank%d_%d" % (j, h), tag="bank%d" % (4 - 4 * h + j))
+                    q_banks[j, h] = bank[:]
                 nc.tensor.matmul_mx(
                     out=q_banks[j, h],
                     lhsT=pj_words[:, 2 * P * j : 2 * P * (j + 1)].bitcast(E2M1),
@@ -193,6 +196,14 @@ def tile_attend_glowmom_pl_kernel(
         def update(j, h, into=None):
             updated[j, h] = sb("updated%d_%d" % (j, h), [P, HALF], F32)[:] if into is None else into
             nc.vector.scalar_tensor_tensor(updated[j, h], picked[j, h], DECAY, q_banks[j, h], MULT, ADD)
+
+        def gather_last(lo, hi, after):
+            picked[3, lo] = sb("picked3_%d" % lo, [P, hi - lo], F32, after=after)[:]
+            scalar_move(picked[3, lo], m_src[3][:].indirect(listed(lo, hi)))
+
+        def update_last(lo, hi, after):
+            updated[3, lo] = sb("updated3_%d" % lo, [P, hi - lo], F32, after=after)[:]
+            nc.vector.scalar_tensor_tensor(updated[3, lo], picked[3, lo], DECAY, q_last[:, lo:hi], MULT, ADD)
 
         def scatter(copy, j, h):
             copy(m_new[j][:].indirect(listed(h * HALF, (h + 1) * HALF)), updated[j, h])
@@ -222,19 +233,19 @@ def tile_attend_glowmom_pl_kernel(
         gather(nc.vector.tensor_copy, 1, 1, after=6592)
         quantize_dw(0)
         second_product(0, (0, 1, 3, 2))
-        gather(scalar_move, 3, 0, after=8192 + 1024 + 64)
+        gather_last(0, LONG, 8192 + 1024 + 64)
         quantize_dw(1)
         update(0, 0, sb("updated0_0", [P, HALF], F32, after=12288)[:])
         scatter(scalar_move, 0, 0)
         second_product(1, (0, 1, 3, 2))
         updated_1 = sb("updated1", [P, SLOTS], F32, after=13312)
         update(1, 0, updated_1[:, half(0)])
-        gather(scalar_move, 3, 1, after=5568)
+        gather_last(LONG, SLOTS, 5568)
         update(0, 1)
         scatter(scalar_move, 0, 1)
         finish_early(0)
         update(1, 1, updated_1[:, half(1)])
-        update(3, 0, sb("updated3_0", [P, HALF], F32, after=3520)[:])
+        update_last(0, LONG, 3008)
         nc.vector.tensor_copy(m_new[1][:].indirect(listed(SHARE, SLOTS)), updated_1[:, SHARE:])
         scalar_move(m_new[1][:].indirect(listed(0, SHARE)), updated_1[:, :SHARE])
         finish_early(1)
@@ -243,11 +254,11 @@ def tile_attend_glowmom_pl_kernel(
         updated_2 = sb("updated2", [P, SLOTS], F32)
         update(2, 0, updated_2[:, half(0)])
         update(2, 1, updated_2[:, half(1)])
-        update(3, 1, sb("updated3_1", [P, HALF], F32, after=6656)[:])
+        update_last(LONG, SLOTS, 6656)
         nc.vector.tensor_copy(m_new[2][:].indirect(offsets[:]), updated_2[:])
         store_lane(2)
-        scatter(scalar_move, 3, 0)
-        scatter(scalar_move, 3, 1)
+        for lo, hi in ((0, LONG), (LONG, SLOTS)):
+            scalar_move(m_new[3][:].indirect(listed(lo, hi)), updated[3, lo])
         store_lane(3)
         nc.vector.tensor_copy(out=pair_lane(2), in_=m_new[2][:])
         for lo, hi in ((0, QUARTER), (QUARTER, COLS)):

@@ -24,7 +24,7 @@ HALF = SLOTS // 2
 QUARTER = COLS // 4
 DECAY = 0.9
 G_SPLIT = 288
-SHARE = 256
+SHARE = 224
 LONG = 384
 FLOPS = 2 * D * R * SLOTS + 2 * K * D * SLOTS
 

@@ -21,7 +21,7 @@ LANES = 4
 D = R = K = SLOTS = 512
 COLS = 1024
 HALF = SLOTS // 2
-QUARTER = COLS // 4
+PIECES = ((0, 128), (128, 384), (384, 640), (640, 1024))
 DECAY = 0.9
 G_SPLIT = 288
 SHARE = 224
@@ -261,33 +261,32 @@ def tile_attend_glowmom_pl_kernel(
             scalar_move(m_new[3][:].indirect(listed(lo, hi)), updated[3, lo])
         store_lane(3)
         nc.vector.tensor_copy(out=pair_lane(2), in_=m_new[2][:])
-        for lo, hi in ((0, QUARTER), (QUARTER, COLS)):
+        first, second, third, widest = PIECES
+        for lo, hi in (first, second, widest, third):
             nc.vector.tensor_copy(out=pair_lane(3)[:, lo:hi], in_=m_new[3][:, lo:hi])
 
-        y_grouped = [sb("y_grouped%d" % s, [P, QUARTER * 2], F32) for s in range(4)]
-        y_codes = [sb("y_codes%d" % s, [P, QUARTER], U32) for s in range(4)]
+        y_grouped = {lo: sb("y_grouped%d" % lo, [P, (hi - lo) * 2], F32) for lo, hi in PIECES}
+        y_codes = {lo: sb("y_codes%d" % lo, [P, hi - lo], U32) for lo, hi in PIECES}
         y_scales = sb("y_scales", [P, COLS], U8)
         words_out = out_1[0].rearrange("p n t -> p (n t)").bitcast(I32)
 
-        def weave(copy, s):
-            cols = slice(s * QUARTER, (s + 1) * QUARTER)
+        def weave(copy, lo, hi):
             copy(
-                out=y_grouped[s][:].rearrange("p (n u) -> p n u", u=2),
-                in_=y_words[:].bitcast(F32)[:, :, cols].rearrange("p u n -> p n u"),
+                out=y_grouped[lo][:].rearrange("p (n u) -> p n u", u=2),
+                in_=y_words[:].bitcast(F32)[:, :, lo:hi].rearrange("p u n -> p n u"),
             )
 
-        def quantize_y(s):
-            cols = slice(s * QUARTER, (s + 1) * QUARTER)
+        def quantize_y(lo, hi):
             nc.vector.quantize_mx(
-                out=y_codes[s][:].bitcast(E4M3), scales=y_scales[:, cols], in_=y_grouped[s][:].bitcast(BF16)
+                out=y_codes[lo][:].bitcast(E4M3), scales=y_scales[:, lo:hi], in_=y_grouped[lo][:].bitcast(BF16)
             )
-            nc.sync.dma_start(out=words_out[:, cols], in_=y_codes[s][:].bitcast(I32))
+            nc.sync.dma_start(out=words_out[:, lo:hi], in_=y_codes[lo][:].bitcast(I32))
 
-        for s in range(3):
-            weave(nc.scalar.copy, s)
-        weave(nc.vector.tensor_copy, 3)
-        for s in (0, 3, 1, 2):
-            quantize_y(s)
+        for lo, hi in (first, second, third):
+            weave(nc.scalar.copy, lo, hi)
+        weave(nc.vector.tensor_copy, *widest)
+        for lo, hi in (first, widest, second, third):
+            quantize_y(lo, hi)
         for q in range(4):
             (nc.scalar, nc.sync)[q % 2].dma_start(
                 out=out_2[0, 4 * q : 4 * q + 4, :].bitcast(I32),

@@ -21,10 +21,10 @@ LANES = 4
 D = R = K = SLOTS = 512
 COLS = 1024
 HALF = SLOTS // 2
-PIECES = ((0, 128), (128, 384), (384, 640), (640, 1024))
+PIECES = ((0, 256), (256, 512), (512, 640), (640, 1024))
 DECAY = 0.9
 G_SPLIT = 288
-SHARE = 224
+SHARE = 256
 LONG = 384
 FLOPS = 2 * D * R * SLOTS + 2 * K * D * SLOTS
 

@@ -288,7 +288,7 @@ def tile_attend_glowmom_pl_kernel(
         for lo, hi in (first, widest, second, third):
             quantize_y(lo, hi)
         for q in range(4):
-            (nc.scalar, nc.sync)[q % 2].dma_start(
+            (nc.scalar if q == 0 else nc.sync).dma_start(
                 out=out_2[0, 4 * q : 4 * q + 4, :].bitcast(I32),
                 in_=y_scales[32 * q : 32 * q + 4, :].bitcast(I32),
             )

@@ -21,7 +21,7 @@ LANES = 4
 D = R = K = SLOTS = 512
 COLS = 1024
 HALF = SLOTS // 2
-PIECES = ((0, 256), (256, 512), (512, 640), (640, 1024))
+PIECES = ((0, 256), (256, 640), (640, 768), (768, 1024))
 DECAY = 0.9
 G_SPLIT = 288
 SHARE = 256
@@ -201,8 +201,8 @@ def tile_attend_glowmom_pl_kernel(
             picked[3, lo] = sb("picked3_%d" % lo, [P, hi - lo], F32, after=after)[:]
             scalar_move(picked[3, lo], m_src[3][:].indirect(listed(lo, hi)))
 
-        def update_last(lo, hi, after):
-            updated[3, lo] = sb("updated3_%d" % lo, [P, hi - lo], F32, after=after)[:]
+        def update_last(lo, hi, into):
+            updated[3, lo] = into
             nc.vector.scalar_tensor_tensor(updated[3, lo], picked[3, lo], DECAY, q_last[:, lo:hi], MULT, ADD)
 
         def scatter(copy, j, h):
@@ -245,7 +245,7 @@ def tile_attend_glowmom_pl_kernel(
         scatter(scalar_move, 0, 1)
         finish_early(0)
         update(1, 1, updated_1[:, half(1)])
-        update_last(0, LONG, 3008)
+        update_last(0, LONG, y_words[:, 1, :].bitcast(F32)[:, COLS - LONG :])
         nc.vector.tensor_copy(m_new[1][:].indirect(listed(SHARE, SLOTS)), updated_1[:, SHARE:])
         scalar_move(m_new[1][:].indirect(listed(0, SHARE)), updated_1[:, :SHARE])
         finish_early(1)
@@ -254,16 +254,22 @@ def tile_attend_glowmom_pl_kernel(
         updated_2 = sb("updated2", [P, SLOTS], F32)
         update(2, 0, updated_2[:, half(0)])
         update(2, 1, updated_2[:, half(1)])
-        update_last(LONG, SLOTS, 6656)
+        update_last(LONG, SLOTS, sb("updated3_b", [P, SLOTS - LONG], F32, after=6656)[:])
         nc.vector.tensor_copy(m_new[2][:].indirect(offsets[:]), updated_2[:])
         store_lane(2)
         for lo, hi in ((0, LONG), (LONG, SLOTS)):
             scalar_move(m_new[3][:].indirect(listed(lo, hi)), updated[3, lo])
         store_lane(3)
-        nc.vector.tensor_copy(out=pair_lane(2), in_=m_new[2][:])
-        first, second, third, widest = PIECES
-        for lo, hi in (first, second, widest, third):
-            nc.vector.tensor_copy(out=pair_lane(3)[:, lo:hi], in_=m_new[3][:, lo:hi])
+        first, widest, third, second = PIECES
+
+        def round_lane(copy, j, lo, hi):
+            copy(out=pair_lane(j)[:, lo:hi], in_=m_new[j][:, lo:hi])
+
+        round_lane(nc.vector.tensor_copy, 2, 0, second[0])
+        for j in (2, 3):
+            round_lane(nc.scalar.copy, j, *second)
+        for lo, hi in (first, widest, third):
+            round_lane(nc.vector.tensor_copy, 3, lo, hi)
 
         y_grouped = {lo: sb("y_grouped%d" % lo, [P, (hi - lo) * 2], F32) for lo, hi in PIECES}
         y_codes = {lo: sb("y_codes%d" % lo, [P, hi - lo], U32) for lo, hi in PIECES}

@@ -24,7 +24,7 @@ HALF = SLOTS // 2
 PIECES = ((0, 256), (256, 640), (640, 768), (768, 1024))
 DECAY = 0.9
 G_SPLIT = 288
-SHARE = 256
+SHARE = 224
 LONG = 384
 FLOPS = 2 * D * R * SLOTS + 2 * K * D * SLOTS
 

from contextlib import ExitStack

import concourse.mybir as mybir
from concourse.masks import make_identity

F32 = mybir.dt.float32
BF16 = mybir.dt.bfloat16
I32 = mybir.dt.int32
U32 = mybir.dt.uint32
U16 = mybir.dt.uint16
U8 = mybir.dt.uint8
E4M3 = mybir.dt.float8_e4m3fn_x4
E5M2 = mybir.dt.float8_e5m2_x4
E2M1 = mybir.dt.float4_e2m1fn_x4
MULT = mybir.AluOpType.mult
ADD = mybir.AluOpType.add
COPY = mybir.ActivationFunctionType.Copy

P = 128
LANES = 4
D = R = K = SLOTS = 512
COLS = 1024
HALF = SLOTS // 2
PIECES = ((0, 256), (256, 640), (640, 768), (768, 1024))
DECAY = 0.9
G_SPLIT = 288
SHARE = 224
LONG = 384
FLOPS = 2 * D * R * SLOTS + 2 * K * D * SLOTS


def tile_attend_glowmom_pl_kernel(
    tc, xT, G, Pj_words, Pj_scales, mT, offs, out_0, out_1, out_2
):
    nc = tc.nc
    with ExitStack() as ctx:
        keep = ctx.enter_context(tc.tile_pool(name="keep", bufs=1))
        shared = ctx.enter_context(tc.tile_pool(name="shared", bufs=1))
        psum = ctx.enter_context(tc.psum_pool(name="psum", bufs=1))

        def sb(name, shape, dtype, after=None):
            if isinstance(after, int):
                return shared.tile(shape, dtype, name=name, offset=after, align_bytes=64)
            return keep.tile(shape, dtype, name=name, tag=after or name, align_bytes=64)

        offsets = keep.tile([P, SLOTS // 16], U16, name="offsets")
        ident = sb("ident", [P, P], F32)
        x_raw = [sb("x_raw%d" % h, [P, 2, R], F32) for h in range(2)]
        g_raw = [sb("g_raw%d" % u, [P, 2, SLOTS], F32) for u in range(2)]
        pj_raw = sb("pj_raw", [P, 2 * K], U8)
        pjs_raw = sb("pjs_raw", [P, K], U8)
        m_src = [sb("m_src%d" % j, [P, COLS], F32) for j in range(LANES)]
        m_new = [sb("m_new%d" % j, [P, COLS], F32) for j in range(LANES)]

        m_rows = mT.rearrange("(p j) t -> p j t", j=LANES)
        out_rows = out_0.rearrange("(p j) t -> p j t", j=LANES)
        g_rows = G.rearrange("(p j) i -> p j i", j=LANES)
        x_rows = xT.rearrange("(p t) r -> p t r", t=LANES)

        nc.gpsimd.memset(pjs_raw[:].bitcast(I32), 0)
        make_identity(nc, ident[:])

        nc.sync.dma_start(out=x_raw[0][:], in_=x_rows[:, 0:2, :])
        nc.sync.dma_start(out=x_raw[1][:], in_=x_rows[:, 2:4, :])
        for q in range(4):
            nc.sync.dma_start(
                out=pjs_raw[32 * q : 32 * q + 4, :].bitcast(I32),
                in_=Pj_scales[0, 4 * q : 4 * q + 4, :].bitcast(I32),
            )
        for u in range(2):
            nc.sync.dma_start(out=g_raw[u][:], in_=g_rows[:, 2 * u : 2 * u + 2, :])
        nc.sync.dma_start(offsets[:], offs)
        nc.sync.dma_start(out=m_src[0][:], in_=m_rows[:, 0, :])
        nc.sync.dma_start(out=pj_raw[:].bitcast(I32), in_=Pj_words[0].bitcast(I32))
        for tiles, j in (
            (m_src, 1), (m_src, 3), (m_new, 0), (m_new, 1), (m_src, 2), (m_new, 2), (m_new, 3)
        ):
            nc.sync.dma_start(out=tiles[j][:], in_=m_rows[:, j, :])

        def half(h):
            return slice(h * HALF, (h + 1) * HALF)

        def block(b):
            return slice(b * P, (b + 1) * P)

        x_codes = sb("x_codes", [P, D], U32)
        x_scales = sb("x_scales", [P, D], U8)
        x_grouped = [sb("x0_grouped", [P, 4 * P], F32, after=3072), sb("x1_grouped", [P, 4 * P], F32)]

        def turn_x(h):
            for c in range(2):
                rounded = sb("x_sorted%d%d" % (h, c), [P, R], BF16)
                nc.vector.tensor_copy(
                    out=rounded[:].rearrange("a (u p e) -> a u p e", u=2, e=2),
                    in_=x_raw[h][:, c, :].rearrange("a (p u e) -> a u p e", u=2, e=2),
                )
                bank = psum.tile([P, 2, P], F32, name="x_bank%d%d" % (h, c), tag="bank%d" % (4 + 2 * h + c))
                words = rounded[:].bitcast(F32)
                for u in range(2):
                    nc.tensor.transpose(bank[:, u, :], words[:, block(u)], ident[:])
                nc.scalar.copy(
                    out=x_grouped[h][:, half(c)].rearrange("p (n u) -> p n u", u=2),
                    in_=bank[:].rearrange("p u n -> p n u"),
                )

        def quantize_x(h):
            nc.vector.quantize_mx(
                out=x_codes[:, half(h)].bitcast(E4M3), scales=x_scales[:, half(h)], in_=x_grouped[h][:].bitcast(BF16)
            )

        turn_x(0)
        pj_scales = sb("pj_scales", [P, K], U8)
        nc.vector.tensor_copy(
            out=pj_scales[:].rearrange("p (j m) -> p j m", j=LANES),
            in_=pjs_raw[:].rearrange("p (m j) -> p j m", j=LANES),
        )
        turn_x(1)
        quantize_x(0)

        g_pieces = ((0, P), (P, HALF), (HALF, SLOTS))
        g_codes = [sb("g_codes%d" % lo, [P, hi - lo], U32) for lo, hi in g_pieces]
        g_scales = [sb("g_scales%d" % lo, [P, hi - lo], U8) for lo, hi in g_pieces]
        g_grouped = [sb("g_grouped%d" % lo, [P, (hi - lo) * LANES], BF16, after=2560 + 8 * lo) for lo, hi in g_pieces]

        def group_g(copy, u, n, lo, hi):
            first = g_pieces[n][0]
            pairs = g_grouped[n][:].rearrange("p (i u e) -> p u i e", u=2, e=2)
            copy(out=pairs[:, u, lo - first : hi - first], in_=g_raw[u][:, :, lo:hi].rearrange("p e i -> p i e"))

        for n, (lo, hi) in enumerate(g_pieces):
            group_g(nc.vector.tensor_copy, 0, n, lo, hi)
        quantize_x(1)
        group_g(nc.scalar.copy, 1, 2, G_SPLIT, SLOTS)
        group_g(nc.vector.tensor_copy, 1, 0, 0, P)
        group_g(nc.vector.tensor_copy, 1, 1, P, HALF)
        group_g(nc.vector.tensor_copy, 1, 2, HALF, G_SPLIT)
        for n in range(3):
            nc.vector.quantize_mx(out=g_codes[n][:].bitcast(E5M2), scales=g_scales[n][:], in_=g_grouped[n][:])

        dw_codes = [sb("dw_codes%d" % h, [P, HALF], U32) for h in range(2)]
        dw_scales = [sb("dw_scales%d" % h, [P, HALF], U8) for h in range(2)]
        dw_grouped = [sb("dw_grouped0", [P, HALF * LANES], BF16, after=8192), sb("dw_grouped1", [P, HALF * LANES], BF16, after=12288)]

        def first_product(b):
            bank = psum.tile([P, LANES, P], F32, name="dw_bank%d" % b, tag="bank%d" % b)
            n, cols = min(b, 2), block(max(b - 2, 0))
            for t in range(LANES):
                nc.tensor.matmul_mx(
                    out=bank[:, t, :],
                    lhsT=x_codes[:, block(t)].bitcast(E4M3),
                    lhsT_scale=x_scales[:, block(t)],
                    rhs=g_codes[n][:, cols].bitcast(E5M2),
                    rhs_scale=g_scales[n][:, cols],
                    start=True,
                    stop=True,
                )
            nc.scalar.copy(
                out=dw_grouped[b // 2][:, b % 2 * SLOTS : (b % 2 + 1) * SLOTS].rearrange("p (n t) -> p n t", t=LANES),
                in_=bank[:].rearrange("p t n -> p n t"),
            )

        q_last = psum.tile([P, SLOTS], F32, name="q_bank3", tag="bank7")
        q_banks = {(3, h): q_last[:, half(h)] for h in range(2)}

        def quantize_dw(h):
            nc.vector.quantize_mx(out=dw_codes[h][:].bitcast(E4M3), scales=dw_scales[h][:], in_=dw_grouped[h][:])

        def second_product(h, lanes):
            for j in lanes:
                if (j, h) not in q_banks:
                    bank = psum.tile([P, HALF], F32, name="q_bank%d_%d" % (j, h), tag="bank%d" % (4 - 4 * h + j))
                    q_banks[j, h] = bank[:]
                nc.tensor.matmul_mx(
                    out=q_banks[j, h],
                    lhsT=pj_words[:, 2 * P * j : 2 * P * (j + 1)].bitcast(E2M1),
                    lhsT_scale=pj_scales[:, block(j)],
                    rhs=dw_codes[h][:].bitcast(E4M3),
                    rhs_scale=dw_scales[h][:],
                    start=True,
                    stop=True,
                )

        picked = {}
        updated = {}

        def listed(lo, hi):
            return offsets[:, lo // 16 : hi // 16]

        def scalar_move(out, in_):
            nc.scalar.activation(out, in_, COPY)

        def gather(copy, j, h, after=None):
            picked[j, h] = sb("picked%d_%d" % (j, h), [P, HALF], F32, after=after)[:]
            copy(picked[j, h], m_src[j][:].indirect(listed(h * HALF, (h + 1) * HALF)))

        def update(j, h, into=None):
            updated[j, h] = sb("updated%d_%d" % (j, h), [P, HALF], F32)[:] if into is None else into
            nc.vector.scalar_tensor_tensor(updated[j, h], picked[j, h], DECAY, q_banks[j, h], MULT, ADD)

        def gather_last(lo, hi, after):
            picked[3, lo] = sb("picked3_%d" % lo, [P, hi - lo], F32, after=after)[:]
            scalar_move(picked[3, lo], m_src[3][:].indirect(listed(lo, hi)))

        def update_last(lo, hi, into):
            updated[3, lo] = into
            nc.vector.scalar_tensor_tensor(updated[3, lo], picked[3, lo], DECAY, q_last[:, lo:hi], MULT, ADD)

        def scatter(copy, j, h):
            copy(m_new[j][:].indirect(listed(h * HALF, (h + 1) * HALF)), updated[j, h])

        y_words = sb("y_words", [P, 2, COLS * 2], BF16)

        def pair_lane(j):
            return y_words[:, j // 2, :].rearrange("p (n e) -> p n e", e=2)[:, :, j % 2]

        def store_lane(j):
            nc.sync.dma_start(out=out_rows[:, j, :], in_=m_new[j][:])

        def finish_early(j):
            store_lane(j)
            nc.gpsimd.tensor_scalar(pair_lane(j), m_new[j][:], 1.0, 0.0, MULT, ADD)

        gather(scalar_move, 0, 0, after=2496)
        for b in range(4):
            first_product(b)
        gather(nc.vector.tensor_copy, 0, 1, after=3520)
        pj_words = sb("pj_words", [P, 2 * K], U8, after=4544)
        nc.vector.tensor_copy(
            out=pj_words[:].bitcast(U16).rearrange("p (j m) -> p j m", j=LANES),
            in_=pj_raw[:].bitcast(U16).rearrange("p (m j) -> p j m", j=LANES),
        )
        gather(nc.vector.tensor_copy, 1, 0, after=5568)
        gather(nc.vector.tensor_copy, 1, 1, after=6592)
        quantize_dw(0)
        second_product(0, (0, 1, 3, 2))
        gather_last(0, LONG, 8192 + 1024 + 64)
        quantize_dw(1)
        update(0, 0, sb("updated0_0", [P, HALF], F32, after=12288)[:])
        scatter(scalar_move, 0, 0)
        second_product(1, (0, 1, 3, 2))
        updated_1 = sb("updated1", [P, SLOTS], F32, after=13312)
        update(1, 0, updated_1[:, half(0)])
        gather_last(LONG, SLOTS, 5568)
        update(0, 1)
        scatter(scalar_move, 0, 1)
        finish_early(0)
        update(1, 1, updated_1[:, half(1)])
        update_last(0, LONG, y_words[:, 1, :].bitcast(F32)[:, COLS - LONG :])
        nc.vector.tensor_copy(m_new[1][:].indirect(listed(SHARE, SLOTS)), updated_1[:, SHARE:])
        scalar_move(m_new[1][:].indirect(listed(0, SHARE)), updated_1[:, :SHARE])
        finish_early(1)
        gather(nc.vector.tensor_copy, 2, 0, after=6656)
        gather(nc.vector.tensor_copy, 2, 1, after=8192 + 1024 + 64)
        updated_2 = sb("updated2", [P, SLOTS], F32)
        update(2, 0, updated_2[:, half(0)])
        update(2, 1, updated_2[:, half(1)])
        update_last(LONG, SLOTS, sb("updated3_b", [P, SLOTS - LONG], F32, after=6656)[:])
        nc.vector.tensor_copy(m_new[2][:].indirect(offsets[:]), updated_2[:])
        store_lane(2)
        for lo, hi in ((0, LONG), (LONG, SLOTS)):
            scalar_move(m_new[3][:].indirect(listed(lo, hi)), updated[3, lo])
        store_lane(3)
        first, widest, third, second = PIECES

        def round_lane(copy, j, lo, hi):
            copy(out=pair_lane(j)[:, lo:hi], in_=m_new[j][:, lo:hi])

        round_lane(nc.vector.tensor_copy, 2, 0, second[0])
        for j in (2, 3):
            round_lane(nc.scalar.copy, j, *second)
        for lo, hi in (first, widest, third):
            round_lane(nc.vector.tensor_copy, 3, lo, hi)

        y_grouped = {lo: sb("y_grouped%d" % lo, [P, (hi - lo) * 2], F32) for lo, hi in PIECES}
        y_codes = {lo: sb("y_codes%d" % lo, [P, hi - lo], U32) for lo, hi in PIECES}
        y_scales = sb("y_scales", [P, COLS], U8)
        words_out = out_1[0].rearrange("p n t -> p (n t)").bitcast(I32)

        def weave(copy, lo, hi):
            copy(
                out=y_grouped[lo][:].rearrange("p (n u) -> p n u", u=2),
                in_=y_words[:].bitcast(F32)[:, :, lo:hi].rearrange("p u n -> p n u"),
            )

        def quantize_y(lo, hi):
            nc.vector.quantize_mx(
                out=y_codes[lo][:].bitcast(E4M3), scales=y_scales[:, lo:hi], in_=y_grouped[lo][:].bitcast(BF16)
            )
            nc.sync.dma_start(out=words_out[:, lo:hi], in_=y_codes[lo][:].bitcast(I32))

        for lo, hi in (first, second, third):
            weave(nc.scalar.copy, lo, hi)
        weave(nc.vector.tensor_copy, *widest)
        for lo, hi in (first, widest, second, third):
            quantize_y(lo, hi)
        for q in range(4):
            (nc.scalar if q == 0 else nc.sync).dma_start(
                out=out_2[0, 4 * q : 4 * q + 4, :].bitcast(I32),
                in_=y_scales[32 * q : 32 * q + 4, :].bitcast(I32),
            )
